import numpy as np
import ml_dtypes


def mxq(x, axis, fmt="e4m3"):
    dtype, down = {"e4m3": (ml_dtypes.float8_e4m3fn, 7), "e5m2": (ml_dtypes.float8_e5m2, 14)}[fmt]
    v = np.moveaxis(np.asarray(x, np.float32).astype(ml_dtypes.bfloat16).astype(np.float64), axis, -1)
    blocks = v.reshape(v.shape[:-1] + (-1, 32))
    amax = np.abs(blocks).max(-1, keepdims=True)
    byte = np.maximum(np.where(amax > 0, np.frexp(amax)[1] - 1 + 127, 0) - down, 1)
    scale = np.exp2(byte - 127.0)
    codes = (blocks / scale).astype(np.float32).astype(dtype).astype(np.float64)
    return np.moveaxis((codes * scale).reshape(v.shape), -1, axis)


WIDE = False


def mx_kscale(k):
    if not WIDE:
        return np.ones(k)
    levels = np.array([10, -10, 5, -5, 0])
    if k % 512:
        return np.exp2(np.random.permutation(np.resize(levels, k // 32))).repeat(32)
    a = np.empty((k // 512, 16))
    for p in range(k // 512):
        a[p, :8] = np.random.permutation(np.resize(levels, 8))
        for g in range(8):
            far = levels[np.abs(levels - a[p, g]) >= 10]
            a[p, g + 8] = far[np.random.randint(len(far))]
    return np.exp2(a.ravel()).repeat(32)


def f64(x):
    return np.asarray(x).astype(np.float64)


def striped(idx):
    return np.tile(idx.reshape(-1, 16).T, (8, 1)).astype(np.uint16)


def unstriped(offs):
    return offs[:16].T.reshape(-1).astype(np.int64)


def striped8(idx):
    return np.concatenate([x.reshape(-1, 16).T for x in idx]).astype(np.uint16)


def runs(offs, k):
    lists = np.stack([offs[16 * r : 16 * r + 16].T.reshape(-1) for r in range(8)]).astype(np.int64)
    return lists[np.arange(k) % 512 // 64]


def pack_weight(w):
    k, n = w.shape
    w = f64(np.asarray(w, np.float32).astype(ml_dtypes.bfloat16)).reshape(k // 32, 32, n)
    amax = np.abs(w).max(1)
    byte = np.clip(np.where(amax > 0, np.frexp(amax)[1] - 1 + 127 - 7, 1), 1, 254)
    scaled = (w * np.exp2(127.0 - byte)[:, None, :]).reshape(k, n).astype(np.float32)
    words = np.ascontiguousarray(scaled.reshape(k // 512, 128, 4, n).transpose(0, 1, 3, 2)).astype(ml_dtypes.float8_e4m3fn).view(np.uint8)
    return words, np.ascontiguousarray(byte.astype(np.uint8).reshape(k // 512, 16, n))


def unpack_weight(words, scales):
    g, p, n, _ = words.shape
    vals = np.ascontiguousarray(words).view(ml_dtypes.float8_e4m3fn).astype(np.float64) * np.repeat(np.exp2(scales.astype(np.float64) - 127.0), 8, axis=1)[..., None]
    return vals.transpose(0, 1, 3, 2).reshape(g * 512, n)


def silu(v):
    return v / (1.0 + np.exp(-np.maximum(v, -700.0)))

def planes(y):
    n, m = y.shape
    v = y.astype(np.float32).astype(ml_dtypes.bfloat16).astype(np.float64).reshape(n // 32, 32, m)
    top = np.abs(v).max(1)
    byte = np.clip(np.where(top > 0, np.frexp(top)[1] - 1 + 127 - 7, 1), 1, 254)
    codes = (v * np.exp2(127.0 - byte)[:, None, :]).reshape(n, m).astype(np.float32).astype(ml_dtypes.float8_e4m3fn).view(np.uint8)
    words = codes.reshape(n // 512, 128, 4, m).transpose(0, 1, 3, 2)
    return np.ascontiguousarray(words), np.ascontiguousarray(byte.astype(np.uint8).reshape(n // 512, 16, m))


K, T, S, N, U, H = 512, 2048, 512, 512, 1024, 512


def setup_inputs():
    n = np.random.standard_normal
    s = mx_kscale(K)[:, None]
    u = mx_kscale(H)
    packed_xT = pack_weight(n((K, T)) * s)
    packed_w2 = pack_weight(n((H, N)) / np.sqrt(H) / u[:, None])
    return {
        "x_words": packed_xT[0],
        "x_scales": packed_xT[1],
        "w1": (n((K, H)) / np.sqrt(K) / s * u).astype(np.float32),
        "mem": (n((H, U)) * u[:, None]).astype(np.float32),
        "w2_words": packed_w2[0],
        "w2_scales": packed_w2[1],
        "offs": striped(np.random.permutation(T)[:S]),
        "slot": striped8(np.stack([np.random.permutation(U)[:S] for _ in range(8)])),
    }


def reference(x_words, x_scales, w1, mem, w2_words, w2_scales, offs, slot):
    xq = unpack_weight(x_words, x_scales)[:, unstriped(offs)]
    y = silu(mxq(f64(w1), 0, "e4m3").T @ xq)
    z = f64(mem).copy()
    z[np.arange(H)[:, None], runs(slot, H)] = y
    out_0 = unpack_weight(w2_words, w2_scales).T @ mxq(z, 0, "e4m3")
    return (out_0,) + planes(out_0)

@@ -1,0 +1,211 @@
+from contextlib import ExitStack
+
+import concourse.mybir as mybir
+
+K, T, S, N, U, H = 512, 2048, 512, 512, 1024, 512
+FLOPS = 2 * K * H * S + 2 * H * N * U
+
+F32 = mybir.dt.float32
+BF16 = mybir.dt.bfloat16
+I32 = mybir.dt.int32
+U32 = mybir.dt.uint32
+U16 = mybir.dt.uint16
+U8 = mybir.dt.uint8
+FP8X4 = mybir.dt.float8_e4m3fn_x4
+SILU = mybir.ActivationFunctionType.Silu
+
+P = 128
+PACK = 4
+QUADS = 4
+BANK = 512
+CHUNK = 256
+CHUNKS = U // CHUNK
+VECTOR_CHUNKS = 2
+UNIT = 128
+UNITS = U // UNIT
+HALF = S // 2
+W1_SPLIT = 80
+
+
+def tile_picked_pagemix_silu_po_kernel(
+    tc, x_words, x_scales, w1, mem, w2_words, w2_scales, offs, slot, out_0, out_1, out_2
+):
+    nc = tc.nc
+    with ExitStack() as ctx:
+        lists = ctx.enter_context(tc.tile_pool(name="lists", bufs=1))
+        keep = ctx.enter_context(tc.tile_pool(name="keep", bufs=1))
+        psum = ctx.enter_context(tc.psum_pool(name="psum", bufs=1))
+
+        offs_t = lists.tile([P, S // 16], U16, name="offs_t")
+        slot_t = lists.tile([P, S // 16], U16, name="slot_t")
+
+        def sb(shape, dtype, name):
+            return keep.tile(shape, dtype, name=name, align_bytes=64)
+
+        def bank(b):
+            return psum.tile([P, BANK], F32, name=f"bank{b}", tag=f"bank{b}")
+
+        x_table = sb([P, T], U32, "x_table")
+        x_scale_table = sb([P, T], U8, "x_scale_table")
+        w1_raw = sb([P, PACK, H], F32, "w1_raw")
+        w2_raw = sb([P, N], U32, "w2_raw")
+        w2_scale_raw = sb([P, N], U8, "w2_scale_raw")
+        page = [sb([P, U], F32, f"page{t}") for t in range(PACK)]
+
+        nc.vector.memset(x_scale_table[:].bitcast(I32), 0)
+        nc.vector.memset(w2_scale_raw[:].bitcast(I32), 0)
+
+        mem_rows = mem.rearrange("(p t) w -> t p w", t=PACK)
+        x_scale_rows = x_scales[0].bitcast(I32)
+        nc.sync.dma_start(offs_t[:], offs)
+        nc.sync.dma_start(w1_raw[:], w1.rearrange("(p j) c -> p j c", j=PACK))
+        for r in range(4):
+            nc.sync.dma_start(x_scale_table[r:P:32, :].bitcast(I32), x_scale_rows[r:16:4, :])
+        nc.sync.dma_start(w2_scale_raw[0:16, :].bitcast(I32), w2_scales[0].bitcast(I32))
+        nc.sync.dma_start(x_table[:].bitcast(I32), x_words[0].rearrange("p n t -> p (n t)").bitcast(I32))
+        nc.sync.dma_start(slot_t[:], slot)
+        nc.sync.dma_start(page[0][:], mem_rows[0])
+        nc.sync.dma_start(w2_raw[:].bitcast(I32), w2_words[0].rearrange("p n t -> p (n t)").bitcast(I32))
+        for t in range(1, PACK):
+            nc.sync.dma_start(page[t][:], mem_rows[t])
+
+        w1_grouped = sb([P, H * PACK], BF16, "w1_grouped")
+        w1_dst = w1_grouped[:].rearrange("p (t m j) -> p m j t", t=PACK, j=PACK)
+        w1_src = w1_raw[:].rearrange("p j (m t) -> p m j t", t=PACK)
+        nc.vector.tensor_copy(out=w1_dst[:, :W1_SPLIT], in_=w1_src[:, :W1_SPLIT])
+        nc.scalar.copy(out=w1_dst[:, W1_SPLIT:], in_=w1_src[:, W1_SPLIT:])
+        w1_codes = sb([P, H], U32, "w1_codes")
+        w1_scale = sb([P, H], U8, "w1_scale")
+        nc.vector.quantize_mx(out=w1_codes[:].bitcast(FP8X4), scales=w1_scale[:], in_=w1_grouped[:])
+        x_scale = sb([P, S], U8, "x_scale")
+        nc.vector.tensor_copy(x_scale[:], x_scale_table[:].indirect(offs_t[:]))
+
+        x_codes = sb([P, S], U32, "x_codes")
+        for h in range(2):
+            nc.vector.tensor_copy(
+                x_codes[:, h * HALF : (h + 1) * HALF],
+                x_table[:].indirect(offs_t[:, h * HALF // 16 : (h + 1) * HALF // 16]),
+            )
+
+        w2_scale = sb([P, N], U8, "w2_scale")
+        nc.vector.tensor_copy(
+            out=w2_scale[:].rearrange("p (t m) -> p m t", t=PACK),
+            in_=w2_scale_raw[:].rearrange("p (m t) -> p m t", t=PACK),
+        )
+        for q in range(1, QUADS):
+            nc.sync.dma_start(
+                w2_scale[32 * q : 32 * q + 4, :].bitcast(I32), w2_scale[4 * q : 4 * q + 4, :].bitcast(I32)
+            )
+
+        y = [sb([P, S], F32, f"y{t}") for t in range(PACK)]
+        pieces = [(0, 0, HALF), (0, HALF, S)] + [(t, 0, S) for t in range(1, PACK)]
+        for b, (t, lo, hi) in enumerate(pieces):
+            acc = bank(7 - b)
+            nc.tensor.matmul_mx(
+                out=acc[:, 0 : hi - lo],
+                lhsT=w1_codes[:, t * P : (t + 1) * P].bitcast(FP8X4),
+                lhsT_scale=w1_scale[:, t * P : (t + 1) * P],
+                rhs=x_codes[:, lo:hi].bitcast(FP8X4),
+                rhs_scale=x_scale[:, lo:hi],
+                start=True,
+                stop=True,
+            )
+            nc.scalar.activation(y[t][:, lo:hi], acc[:, 0 : hi - lo], SILU)
+
+        w2_codes = sb([P, N], U32, "w2_codes")
+        z_grouped = [sb([P, CHUNK, PACK], BF16, f"z_grouped{c}") for c in range(CHUNKS)]
+        for b, (t, lo, hi) in enumerate(pieces):
+            nc.vector.tensor_copy(page[t][:].indirect(slot_t[:, lo // 16 : hi // 16]), y[t][:, lo:hi])
+            if b == 0:
+                nc.vector.tensor_copy(
+                    out=w2_codes[:].bitcast(I32).rearrange("p (t m) -> p m t", t=PACK),
+                    in_=w2_raw[:].bitcast(I32).rearrange("p (m t) -> p m t", t=PACK),
+                )
+            if hi < S or t == PACK - 1:
+                continue
+            for c in range(CHUNKS):
+                cols = page[t][:, c * CHUNK : (c + 1) * CHUNK]
+                if t == PACK - 2 and c < VECTOR_CHUNKS:
+                    nc.scalar.copy(
+                        out=z_grouped[c][:, :, t : t + 2],
+                        in_=cols.rearrange("p (w o) -> p w o", o=1).to_broadcast([P, CHUNK, 2]),
+                    )
+                else:
+                    nc.scalar.copy(out=z_grouped[c][:, :, t], in_=cols)
+
+        last = PACK - 1
+        z_codes = sb([P, U], U32, "z_codes")
+        z_scale = sb([P, U], U8, "z_scale")
+
+        def z_part(lo, hi):
+            c = lo // CHUNK
+            return z_grouped[c][:, lo - c * CHUNK : hi - c * CHUNK, :]
+
+        def round_last(lo, hi):
+            engine_copy = nc.vector.tensor_copy if lo < VECTOR_CHUNKS * CHUNK else nc.scalar.copy
+            engine_copy(out=z_part(lo, hi)[:, :, last], in_=page[last][:, lo:hi])
+
+        def quantise_z(lo, hi):
+            nc.vector.quantize_mx(
+                out=z_codes[:, lo:hi].bitcast(FP8X4),
+                scales=z_scale[:, lo:hi],
+                in_=z_part(lo, hi).rearrange("p w t -> p (w t)"),
+            )
+
+        parts = [(0, UNIT), (UNIT, CHUNK)] + [(c * CHUNK, (c + 1) * CHUNK) for c in range(1, CHUNKS)]
+        round_last(*parts[0])
+        for i, part in enumerate(parts):
+            if i + 1 < len(parts):
+                round_last(*parts[i + 1])
+            quantise_z(*part)
+
+        out_rows = out_0.rearrange("(p t) w -> p t w", t=PACK)
+        out_words = out_1[0].rearrange("p n t -> p (n t)").bitcast(I32)
+        o_codes = sb([P, U], U32, "o_codes")
+        o_scale = sb([P, U], U8, "o_scale")
+        result = [sb([P, PACK, CHUNK], F32, f"result{c}") for c in range(CHUNKS)]
+        o_grouped = [sb([P, CHUNK, PACK], BF16, f"o_grouped{c}") for c in range(CHUNKS)]
+
+        def quantise_out(lo, hi):
+            c = lo // CHUNK
+            nc.vector.quantize_mx(
+                out=o_codes[:, lo:hi].bitcast(FP8X4),
+                scales=o_scale[:, lo:hi],
+                in_=o_grouped[c][:, lo - c * CHUNK : hi - c * CHUNK, :].rearrange("p w t -> p (w t)"),
+            )
+            nc.sync.dma_start(out_words[:, lo:hi], o_codes[:, lo:hi].bitcast(I32))
+
+        for u in range(UNITS):
+            c, inside = divmod(u * UNIT, CHUNK)
+            cs = slice(u * UNIT, (u + 1) * UNIT)
+            local = slice(inside, inside + UNIT)
+            acc = bank(u)
+            for t in range(PACK):
+                nc.tensor.matmul_mx(
+                    out=acc[:, t * UNIT : (t + 1) * UNIT],
+                    lhsT=w2_codes[:, t * P : (t + 1) * P].bitcast(FP8X4),
+                    lhsT_scale=w2_scale[:, t * P : (t + 1) * P],
+                    rhs=z_codes[:, cs].bitcast(FP8X4),
+                    rhs_scale=z_scale[:, cs],
+                    start=True,
+                    stop=True,
+                )
+            nc.scalar.copy(out=result[c][:, :, local], in_=acc[:].rearrange("p (t w) -> p t w", t=PACK))
+            if c == 0:
+                nc.sync.dma_start(out_rows[:, :, cs], result[c][:, :, local])
+            elif inside:
+                nc.sync.dma_start(out_rows[:, :, c * CHUNK : (c + 1) * CHUNK], result[c][:])
+            nc.vector.tensor_copy(
+                out=o_grouped[c][:, local, :].rearrange("p (c i) t -> p c t i", i=4),
+                in_=result[c][:, :, local].rearrange("p t (c i) -> p c t i", i=4),
+            )
+            if u >= 2 and u % 2 == 0:
+                quantise_out((u - 2) * UNIT, u * UNIT)
+            if u == UNITS - 1:
+                quantise_out((u - 1) * UNIT, u * UNIT)
+                quantise_out(u * UNIT, (u + 1) * UNIT)
+
+        out_scale_rows = out_2[0].bitcast(I32)
+        for r in range(4):
+            queue = nc.sync if r < 2 else nc.scalar
+            queue.dma_start(out_scale_rows[r:16:4, :], o_scale[r:P:32, :].bitcast(I32))

@@ -24,7 +24,7 @@ VECTOR_CHUNKS = 2
 UNIT = 128
 UNITS = U // UNIT
 HALF = S // 2
-W1_SPLIT = 80
+W1_SPLIT = 64
 
 
 def tile_picked_pagemix_silu_po_kernel(
@@ -52,8 +52,8 @@ def tile_picked_pagemix_silu_po_kernel(
         w2_scale_raw = sb([P, N], U8, "w2_scale_raw")
         page = [sb([P, U], F32, f"page{t}") for t in range(PACK)]
 
-        nc.vector.memset(x_scale_table[:].bitcast(I32), 0)
         nc.vector.memset(w2_scale_raw[:].bitcast(I32), 0)
+        nc.vector.memset(x_scale_table[:].bitcast(I32), 0)
 
         mem_rows = mem.rearrange("(p t) w -> t p w", t=PACK)
         x_scale_rows = x_scales[0].bitcast(I32)
@@ -61,14 +61,20 @@ def tile_picked_pagemix_silu_po_kernel(
         nc.sync.dma_start(w1_raw[:], w1.rearrange("(p j) c -> p j c", j=PACK))
         for r in range(4):
             nc.sync.dma_start(x_scale_table[r:P:32, :].bitcast(I32), x_scale_rows[r:16:4, :])
-        nc.sync.dma_start(w2_scale_raw[0:16, :].bitcast(I32), w2_scales[0].bitcast(I32))
+        nc.scalar.dma_start(w2_scale_raw[0:16, :].bitcast(I32), w2_scales[0].bitcast(I32))
         nc.sync.dma_start(x_table[:].bitcast(I32), x_words[0].rearrange("p n t -> p (n t)").bitcast(I32))
         nc.sync.dma_start(slot_t[:], slot)
         nc.sync.dma_start(page[0][:], mem_rows[0])
+        nc.sync.dma_start(page[1][:], mem_rows[1])
         nc.sync.dma_start(w2_raw[:].bitcast(I32), w2_words[0].rearrange("p n t -> p (n t)").bitcast(I32))
-        for t in range(1, PACK):
+        for t in range(2, PACK):
             nc.sync.dma_start(page[t][:], mem_rows[t])
 
+        w2_scale = sb([P, N], U8, "w2_scale")
+        nc.vector.tensor_copy(
+            out=w2_scale[:].rearrange("p (t m) -> p m t", t=PACK),
+            in_=w2_scale_raw[:].rearrange("p (m t) -> p m t", t=PACK),
+        )
         w1_grouped = sb([P, H * PACK], BF16, "w1_grouped")
         w1_dst = w1_grouped[:].rearrange("p (t m j) -> p m j t", t=PACK, j=PACK)
         w1_src = w1_raw[:].rearrange("p j (m t) -> p m j t", t=PACK)
@@ -87,11 +93,6 @@ def tile_picked_pagemix_silu_po_kernel(
                 x_table[:].indirect(offs_t[:, h * HALF // 16 : (h + 1) * HALF // 16]),
             )
 
-        w2_scale = sb([P, N], U8, "w2_scale")
-        nc.vector.tensor_copy(
-            out=w2_scale[:].rearrange("p (t m) -> p m t", t=PACK),
-            in_=w2_scale_raw[:].rearrange("p (m t) -> p m t", t=PACK),
-        )
         for q in range(1, QUADS):
             nc.sync.dma_start(
                 w2_scale[32 * q : 32 * q + 4, :].bitcast(I32), w2_scale[4 * q : 4 * q + 4, :].bitcast(I32)

@@ -114,7 +114,8 @@ def tile_picked_pagemix_silu_po_kernel(
             nc.scalar.activation(y[t][:, lo:hi], acc[:, 0 : hi - lo], SILU)
 
         w2_codes = sb([P, N], U32, "w2_codes")
-        z_grouped = [sb([P, CHUNK, PACK], BF16, f"z_grouped{c}") for c in range(CHUNKS)]
+        z_grouped = sb([P, U, PACK], BF16, "z_grouped")
+        parts = [(0, UNIT), (UNIT, CHUNK)] + [(c * CHUNK, (c + 1) * CHUNK) for c in range(1, CHUNKS)]
         for b, (t, lo, hi) in enumerate(pieces):
             nc.vector.tensor_copy(page[t][:].indirect(slot_t[:, lo // 16 : hi // 16]), y[t][:, lo:hi])
             if b == 0:
@@ -124,23 +125,25 @@ def tile_picked_pagemix_silu_po_kernel(
                 )
             if hi < S or t == PACK - 1:
                 continue
-            for c in range(CHUNKS):
-                cols = page[t][:, c * CHUNK : (c + 1) * CHUNK]
-                if t == PACK - 2 and c < VECTOR_CHUNKS:
-                    nc.scalar.copy(
-                        out=z_grouped[c][:, :, t : t + 2],
-                        in_=cols.rearrange("p (w o) -> p w o", o=1).to_broadcast([P, CHUNK, 2]),
-                    )
-                else:
-                    nc.scalar.copy(out=z_grouped[c][:, :, t], in_=cols)
+            if t < PACK - 2:
+                nc.scalar.copy(out=z_grouped[:, :, t], in_=page[t][:])
+                continue
+            for first, end in parts:
+                if first >= VECTOR_CHUNKS * CHUNK:
+                    nc.scalar.copy(out=z_grouped[:, first:end, t], in_=page[t][:, first:end])
+                    continue
+                nc.scalar.copy(out=z_grouped[:, first : end - 2, t], in_=page[t][:, first : end - 2])
+                nc.scalar.copy(
+                    out=z_grouped[:, end - 2 : end, t : t + 2],
+                    in_=page[t][:, end - 2 : end].rearrange("p (w o) -> p w o", o=1).to_broadcast([P, 2, 2]),
+                )
 
         last = PACK - 1
         z_codes = sb([P, U], U32, "z_codes")
         z_scale = sb([P, U], U8, "z_scale")
 
         def z_part(lo, hi):
-            c = lo // CHUNK
-            return z_grouped[c][:, lo - c * CHUNK : hi - c * CHUNK, :]
+            return z_grouped[:, lo:hi, :]
 
         def round_last(lo, hi):
             engine_copy = nc.vector.tensor_copy if lo < VECTOR_CHUNKS * CHUNK else nc.scalar.copy
@@ -153,7 +156,6 @@ def tile_picked_pagemix_silu_po_kernel(
                 in_=z_part(lo, hi).rearrange("p w t -> p (w t)"),
             )
 
-        parts = [(0, UNIT), (UNIT, CHUNK)] + [(c * CHUNK, (c + 1) * CHUNK) for c in range(1, CHUNKS)]
         round_last(*parts[0])
         for i, part in enumerate(parts):
             if i + 1 < len(parts):
@@ -196,15 +198,16 @@ def tile_picked_pagemix_silu_po_kernel(
                 nc.sync.dma_start(out_rows[:, :, cs], result[c][:, :, local])
             elif inside:
                 nc.sync.dma_start(out_rows[:, :, c * CHUNK : (c + 1) * CHUNK], result[c][:])
-            nc.vector.tensor_copy(
-                out=o_grouped[c][:, local, :].rearrange("p (c i) t -> p c t i", i=4),
-                in_=result[c][:, :, local].rearrange("p t (c i) -> p c t i", i=4),
-            )
+            if u == UNITS - 1:
+                nc.scalar.copy(out=o_grouped[c][:, local, :], in_=acc[:].rearrange("p (t w) -> p w t", t=PACK))
+            if u < UNITS - 1:
+                nc.vector.tensor_copy(
+                    out=o_grouped[c][:, local, :].rearrange("p (c i) t -> p c t i", i=4),
+                    in_=result[c][:, :, local].rearrange("p t (c i) -> p c t i", i=4),
+                )
             if u >= 2 and u % 2 == 0:
                 quantise_out((u - 2) * UNIT, u * UNIT)
-            if u == UNITS - 1:
-                quantise_out((u - 1) * UNIT, u * UNIT)
-                quantise_out(u * UNIT, (u + 1) * UNIT)
+        quantise_out(U - CHUNK, U)
 
         out_scale_rows = out_2[0].bitcast(I32)
         for r in range(4):

@@ -24,6 +24,7 @@ VECTOR_CHUNKS = 2
 UNIT = 128
 UNITS = U // UNIT
 HALF = S // 2
+FIRST = 128
 W1_SPLIT = 64
 
 
@@ -82,7 +83,14 @@ def tile_picked_pagemix_silu_po_kernel(
         nc.scalar.copy(out=w1_dst[:, W1_SPLIT:], in_=w1_src[:, W1_SPLIT:])
         w1_codes = sb([P, H], U32, "w1_codes")
         w1_scale = sb([P, H], U8, "w1_scale")
-        nc.vector.quantize_mx(out=w1_codes[:].bitcast(FP8X4), scales=w1_scale[:], in_=w1_grouped[:])
+        def quantise_w1(lo, hi):
+            nc.vector.quantize_mx(
+                out=w1_codes[:, lo:hi].bitcast(FP8X4),
+                scales=w1_scale[:, lo:hi],
+                in_=w1_grouped[:, lo * PACK : hi * PACK],
+            )
+
+        quantise_w1(0, P)
         x_scale = sb([P, S], U8, "x_scale")
         nc.vector.tensor_copy(x_scale[:], x_scale_table[:].indirect(offs_t[:]))
 
@@ -93,25 +101,29 @@ def tile_picked_pagemix_silu_po_kernel(
                 x_table[:].indirect(offs_t[:, h * HALF // 16 : (h + 1) * HALF // 16]),
             )
 
+        quantise_w1(P, 2 * P)
+        quantise_w1(2 * P, H)
         for q in range(1, QUADS):
             nc.sync.dma_start(
                 w2_scale[32 * q : 32 * q + 4, :].bitcast(I32), w2_scale[4 * q : 4 * q + 4, :].bitcast(I32)
             )
 
         y = [sb([P, S], F32, f"y{t}") for t in range(PACK)]
-        pieces = [(0, 0, HALF), (0, HALF, S)] + [(t, 0, S) for t in range(1, PACK)]
+        pieces = [(0, 0, FIRST), (0, FIRST, S)] + [(t, 0, S) for t in range(1, PACK)]
         for b, (t, lo, hi) in enumerate(pieces):
             acc = bank(7 - b)
-            nc.tensor.matmul_mx(
-                out=acc[:, 0 : hi - lo],
-                lhsT=w1_codes[:, t * P : (t + 1) * P].bitcast(FP8X4),
-                lhsT_scale=w1_scale[:, t * P : (t + 1) * P],
-                rhs=x_codes[:, lo:hi].bitcast(FP8X4),
-                rhs_scale=x_scale[:, lo:hi],
-                start=True,
-                stop=True,
-            )
-            nc.scalar.activation(y[t][:, lo:hi], acc[:, 0 : hi - lo], SILU)
+            cuts = [lo, HALF, hi] if lo == FIRST else [lo, hi]
+            for first, end in zip(cuts, cuts[1:]):
+                nc.tensor.matmul_mx(
+                    out=acc[:, first:end],
+                    lhsT=w1_codes[:, t * P : (t + 1) * P].bitcast(FP8X4),
+                    lhsT_scale=w1_scale[:, t * P : (t + 1) * P],
+                    rhs=x_codes[:, first:end].bitcast(FP8X4),
+                    rhs_scale=x_scale[:, first:end],
+                    start=True,
+                    stop=True,
+                )
+            nc.scalar.activation(y[t][:, lo:hi], acc[:, lo:hi], SILU)
 
         w2_codes = sb([P, N], U32, "w2_codes")
         z_grouped = sb([P, U, PACK], BF16, "z_grouped")

@@ -20,12 +20,13 @@ QUADS = 4
 BANK = 512
 CHUNK = 256
 CHUNKS = U // CHUNK
-VECTOR_CHUNKS = 2
 UNIT = 128
 UNITS = U // UNIT
 HALF = S // 2
 FIRST = 128
-W1_SPLIT = 64
+W1_HALF = 64
+VECTOR_SLOTS = 640
+ORDER = (0, 1, 2, 3)
 
 
 def tile_picked_pagemix_silu_po_kernel(
@@ -40,35 +41,36 @@ def tile_picked_pagemix_silu_po_kernel(
         offs_t = lists.tile([P, S // 16], U16, name="offs_t")
         slot_t = lists.tile([P, S // 16], U16, name="slot_t")
 
-        def sb(shape, dtype, name):
-            return keep.tile(shape, dtype, name=name, align_bytes=64)
+        def sb(shape, dtype, name, tag=None):
+            return keep.tile(shape, dtype, name=name, tag=tag or name, align_bytes=64)
 
         def bank(b):
             return psum.tile([P, BANK], F32, name=f"bank{b}", tag=f"bank{b}")
 
         x_table = sb([P, T], U32, "x_table")
         x_scale_table = sb([P, T], U8, "x_scale_table")
-        w1_raw = sb([P, PACK, H], F32, "w1_raw")
+        w1_raw = [sb([P, PACK, H // 2], F32, f"w1_raw{h}") for h in range(2)]
         w2_raw = sb([P, N], U32, "w2_raw")
         w2_scale_raw = sb([P, N], U8, "w2_scale_raw")
         page = [sb([P, U], F32, f"page{t}") for t in range(PACK)]
 
-        nc.vector.memset(w2_scale_raw[:].bitcast(I32), 0)
         nc.vector.memset(x_scale_table[:].bitcast(I32), 0)
+        nc.vector.memset(w2_scale_raw[:].bitcast(I32), 0)
 
         mem_rows = mem.rearrange("(p t) w -> t p w", t=PACK)
+        w1_rows = w1.rearrange("(p j) c -> p j c", j=PACK)
         x_scale_rows = x_scales[0].bitcast(I32)
         nc.sync.dma_start(offs_t[:], offs)
-        nc.sync.dma_start(w1_raw[:], w1.rearrange("(p j) c -> p j c", j=PACK))
+        nc.sync.dma_start(w1_raw[0][:], w1_rows[:, :, : H // 2])
         for r in range(4):
             nc.sync.dma_start(x_scale_table[r:P:32, :].bitcast(I32), x_scale_rows[r:16:4, :])
+        nc.sync.dma_start(w1_raw[1][:], w1_rows[:, :, H // 2 :])
         nc.scalar.dma_start(w2_scale_raw[0:16, :].bitcast(I32), w2_scales[0].bitcast(I32))
         nc.sync.dma_start(x_table[:].bitcast(I32), x_words[0].rearrange("p n t -> p (n t)").bitcast(I32))
         nc.sync.dma_start(slot_t[:], slot)
-        nc.sync.dma_start(page[0][:], mem_rows[0])
-        nc.sync.dma_start(page[1][:], mem_rows[1])
+        nc.sync.dma_start(page[ORDER[0]][:], mem_rows[ORDER[0]])
         nc.sync.dma_start(w2_raw[:].bitcast(I32), w2_words[0].rearrange("p n t -> p (n t)").bitcast(I32))
-        for t in range(2, PACK):
+        for t in ORDER[1:]:
             nc.sync.dma_start(page[t][:], mem_rows[t])
 
         w2_scale = sb([P, N], U8, "w2_scale")
@@ -78,21 +80,14 @@ def tile_picked_pagemix_silu_po_kernel(
         )
         w1_grouped = sb([P, H * PACK], BF16, "w1_grouped")
         w1_dst = w1_grouped[:].rearrange("p (t m j) -> p m j t", t=PACK, j=PACK)
-        w1_src = w1_raw[:].rearrange("p j (m t) -> p m j t", t=PACK)
-        nc.vector.tensor_copy(out=w1_dst[:, :W1_SPLIT], in_=w1_src[:, :W1_SPLIT])
-        nc.scalar.copy(out=w1_dst[:, W1_SPLIT:], in_=w1_src[:, W1_SPLIT:])
-        w1_codes = sb([P, H], U32, "w1_codes")
-        w1_scale = sb([P, H], U8, "w1_scale")
-        def quantise_w1(lo, hi):
-            nc.vector.quantize_mx(
-                out=w1_codes[:, lo:hi].bitcast(FP8X4),
-                scales=w1_scale[:, lo:hi],
-                in_=w1_grouped[:, lo * PACK : hi * PACK],
-            )
-
-        quantise_w1(0, P)
+        w1_src = [w1_raw[h][:].rearrange("p j (m t) -> p m j t", t=PACK) for h in range(2)]
+        nc.scalar.copy(out=w1_dst[:, :W1_HALF], in_=w1_src[0])
         x_scale = sb([P, S], U8, "x_scale")
         nc.vector.tensor_copy(x_scale[:], x_scale_table[:].indirect(offs_t[:]))
+        nc.vector.tensor_copy(out=w1_dst[:, W1_HALF:], in_=w1_src[1])
+        w1_codes = sb([P, H], U32, "w1_codes")
+        w1_scale = sb([P, H], U8, "w1_scale")
+        nc.vector.quantize_mx(out=w1_codes[:].bitcast(FP8X4), scales=w1_scale[:], in_=w1_grouped[:])
 
         x_codes = sb([P, S], U32, "x_codes")
         for h in range(2):
@@ -101,103 +96,98 @@ def tile_picked_pagemix_silu_po_kernel(
                 x_table[:].indirect(offs_t[:, h * HALF // 16 : (h + 1) * HALF // 16]),
             )
 
-        quantise_w1(P, 2 * P)
-        quantise_w1(2 * P, H)
         for q in range(1, QUADS):
             nc.sync.dma_start(
                 w2_scale[32 * q : 32 * q + 4, :].bitcast(I32), w2_scale[4 * q : 4 * q + 4, :].bitcast(I32)
             )
 
-        y = [sb([P, S], F32, f"y{t}") for t in range(PACK)]
-        pieces = [(0, 0, FIRST), (0, FIRST, S)] + [(t, 0, S) for t in range(1, PACK)]
-        for b, (t, lo, hi) in enumerate(pieces):
-            acc = bank(7 - b)
-            cuts = [lo, HALF, hi] if lo == FIRST else [lo, hi]
-            for first, end in zip(cuts, cuts[1:]):
-                nc.tensor.matmul_mx(
-                    out=acc[:, first:end],
-                    lhsT=w1_codes[:, t * P : (t + 1) * P].bitcast(FP8X4),
-                    lhsT_scale=w1_scale[:, t * P : (t + 1) * P],
-                    rhs=x_codes[:, first:end].bitcast(FP8X4),
-                    rhs_scale=x_scale[:, first:end],
-                    start=True,
-                    stop=True,
-                )
-            nc.scalar.activation(y[t][:, lo:hi], acc[:, lo:hi], SILU)
-
         w2_codes = sb([P, N], U32, "w2_codes")
         z_grouped = sb([P, U, PACK], BF16, "z_grouped")
-        parts = [(0, UNIT), (UNIT, CHUNK)] + [(c * CHUNK, (c + 1) * CHUNK) for c in range(1, CHUNKS)]
-        for b, (t, lo, hi) in enumerate(pieces):
-            nc.vector.tensor_copy(page[t][:].indirect(slot_t[:, lo // 16 : hi // 16]), y[t][:, lo:hi])
-            if b == 0:
-                nc.vector.tensor_copy(
-                    out=w2_codes[:].bitcast(I32).rearrange("p (t m) -> p m t", t=PACK),
-                    in_=w2_raw[:].bitcast(I32).rearrange("p (m t) -> p m t", t=PACK),
-                )
-            if hi < S or t == PACK - 1:
-                continue
-            if t < PACK - 2:
-                nc.scalar.copy(out=z_grouped[:, :, t], in_=page[t][:])
-                continue
-            for first, end in parts:
-                if first >= VECTOR_CHUNKS * CHUNK:
-                    nc.scalar.copy(out=z_grouped[:, first:end, t], in_=page[t][:, first:end])
-                    continue
-                nc.scalar.copy(out=z_grouped[:, first : end - 2, t], in_=page[t][:, first : end - 2])
-                nc.scalar.copy(
-                    out=z_grouped[:, end - 2 : end, t : t + 2],
-                    in_=page[t][:, end - 2 : end].rearrange("p (w o) -> p w o", o=1).to_broadcast([P, 2, 2]),
-                )
+        last = ORDER[-1]
 
-        last = PACK - 1
+        def product(t, acc, lo, hi):
+            nc.tensor.matmul_mx(
+                out=acc[:, lo:hi],
+                lhsT=w1_codes[:, t * P : (t + 1) * P].bitcast(FP8X4),
+                lhsT_scale=w1_scale[:, t * P : (t + 1) * P],
+                rhs=x_codes[:, lo:hi].bitcast(FP8X4),
+                rhs_scale=x_scale[:, lo:hi],
+                start=True,
+                stop=True,
+            )
+
+        def scatter(t, y, lo, hi):
+            nc.vector.tensor_copy(page[t][:].indirect(slot_t[:, lo // 16 : hi // 16]), y[:, lo:hi])
+
+        first = ORDER[0]
+        y = {t: sb([P, S], F32, f"y{t}") for t in ORDER}
+        acc = bank(7)
+        product(first, acc, 0, FIRST)
+        nc.scalar.activation(y[first][:, :FIRST], acc[:, :FIRST], SILU)
+        acc = bank(6)
+        product(first, acc, FIRST, HALF)
+        product(first, acc, HALF, S)
+        nc.scalar.activation(y[first][:, FIRST:], acc[:, FIRST:], SILU)
+        accs = {}
+        for b, t in enumerate(ORDER[1:]):
+            accs[t] = bank(5 - b)
+            product(t, accs[t], 0, S)
+            nc.scalar.activation(y[t][:], accs[t][:], SILU)
+
+        scatter(first, y[first], 0, FIRST)
+        nc.vector.tensor_copy(
+            out=w2_codes[:].bitcast(I32).rearrange("p (t m) -> p m t", t=PACK),
+            in_=w2_raw[:].bitcast(I32).rearrange("p (m t) -> p m t", t=PACK),
+        )
+        scatter(first, y[first], FIRST, S)
+        nc.scalar.copy(out=z_grouped[:, :, first], in_=page[first][:])
+        for t in ORDER[1:]:
+            scatter(t, y[t], 0, S)
+            if t == ORDER[1]:
+                nc.scalar.copy(out=z_grouped[:, :, t], in_=page[t][:])
+            if t == ORDER[2]:
+                for lo, hi in ((0, CHUNK), (CHUNK, 2 * CHUNK), (2 * CHUNK, VECTOR_SLOTS)):
+                    nc.scalar.copy(
+                        out=z_grouped[:, lo:hi, t : t + 2],
+                        in_=page[t][:, lo:hi].rearrange("p (w o) -> p w o", o=1).to_broadcast([P, hi - lo, 2]),
+                    )
+                nc.scalar.copy(out=z_grouped[:, VECTOR_SLOTS:, t], in_=page[t][:, VECTOR_SLOTS:])
+
         z_codes = sb([P, U], U32, "z_codes")
         z_scale = sb([P, U], U8, "z_scale")
 
-        def z_part(lo, hi):
-            return z_grouped[:, lo:hi, :]
-
-        def round_last(lo, hi):
-            engine_copy = nc.vector.tensor_copy if lo < VECTOR_CHUNKS * CHUNK else nc.scalar.copy
-            engine_copy(out=z_part(lo, hi)[:, :, last], in_=page[last][:, lo:hi])
+        def round_last(engine_copy, lo, hi):
+            engine_copy(out=z_grouped[:, lo:hi, last], in_=page[last][:, lo:hi])
 
         def quantise_z(lo, hi):
             nc.vector.quantize_mx(
                 out=z_codes[:, lo:hi].bitcast(FP8X4),
                 scales=z_scale[:, lo:hi],
-                in_=z_part(lo, hi).rearrange("p w t -> p (w t)"),
+                in_=z_grouped[:, lo:hi, :].rearrange("p w t -> p (w t)"),
             )
 
-        round_last(*parts[0])
-        for i, part in enumerate(parts):
-            if i + 1 < len(parts):
-                round_last(*parts[i + 1])
-            quantise_z(*part)
+        round_last(nc.vector.tensor_copy, 0, UNIT)
+        round_last(nc.vector.tensor_copy, UNIT, CHUNK)
+        round_last(nc.scalar.copy, VECTOR_SLOTS, U)
+        quantise_z(0, UNIT)
+        round_last(nc.vector.tensor_copy, CHUNK, 2 * CHUNK)
+        quantise_z(UNIT, CHUNK)
+        round_last(nc.vector.tensor_copy, 2 * CHUNK, VECTOR_SLOTS)
+        quantise_z(CHUNK, 2 * CHUNK)
+        quantise_z(2 * CHUNK, U)
 
         out_rows = out_0.rearrange("(p t) w -> p t w", t=PACK)
         out_words = out_1[0].rearrange("p n t -> p (n t)").bitcast(I32)
         o_codes = sb([P, U], U32, "o_codes")
         o_scale = sb([P, U], U8, "o_scale")
-        result = [sb([P, PACK, CHUNK], F32, f"result{c}") for c in range(CHUNKS)]
-        o_grouped = [sb([P, CHUNK, PACK], BF16, f"o_grouped{c}") for c in range(CHUNKS)]
+        result = sb([P, PACK, U], F32, "result")
+        o_grouped = sb([P, U, PACK], BF16, "o_grouped")
 
-        def quantise_out(lo, hi):
-            c = lo // CHUNK
-            nc.vector.quantize_mx(
-                out=o_codes[:, lo:hi].bitcast(FP8X4),
-                scales=o_scale[:, lo:hi],
-                in_=o_grouped[c][:, lo - c * CHUNK : hi - c * CHUNK, :].rearrange("p w t -> p (w t)"),
-            )
-            nc.sync.dma_start(out_words[:, lo:hi], o_codes[:, lo:hi].bitcast(I32))
-
-        for u in range(UNITS):
-            c, inside = divmod(u * UNIT, CHUNK)
+        def mix(acc, planes, u):
             cs = slice(u * UNIT, (u + 1) * UNIT)
-            local = slice(inside, inside + UNIT)
-            acc = bank(u)
-            for t in range(PACK):
+            for i, t in enumerate(planes):
                 nc.tensor.matmul_mx(
-                    out=acc[:, t * UNIT : (t + 1) * UNIT],
+                    out=acc[:, i * UNIT : (i + 1) * UNIT],
                     lhsT=w2_codes[:, t * P : (t + 1) * P].bitcast(FP8X4),
                     lhsT_scale=w2_scale[:, t * P : (t + 1) * P],
                     rhs=z_codes[:, cs].bitcast(FP8X4),
@@ -205,23 +195,67 @@ def tile_picked_pagemix_silu_po_kernel(
                     start=True,
                     stop=True,
                 )
-            nc.scalar.copy(out=result[c][:, :, local], in_=acc[:].rearrange("p (t w) -> p t w", t=PACK))
-            if c == 0:
-                nc.sync.dma_start(out_rows[:, :, cs], result[c][:, :, local])
-            elif inside:
-                nc.sync.dma_start(out_rows[:, :, c * CHUNK : (c + 1) * CHUNK], result[c][:])
-            if u == UNITS - 1:
-                nc.scalar.copy(out=o_grouped[c][:, local, :], in_=acc[:].rearrange("p (t w) -> p w t", t=PACK))
-            if u < UNITS - 1:
-                nc.vector.tensor_copy(
-                    out=o_grouped[c][:, local, :].rearrange("p (c i) t -> p c t i", i=4),
-                    in_=result[c][:, :, local].rearrange("p t (c i) -> p c t i", i=4),
-                )
-            if u >= 2 and u % 2 == 0:
-                quantise_out((u - 2) * UNIT, u * UNIT)
-        quantise_out(U - CHUNK, U)
 
+        def copy_out(acc, ts, u):
+            n = ts.stop - ts.start
+            nc.scalar.copy(
+                out=result[:, ts, u * UNIT : (u + 1) * UNIT],
+                in_=acc[:, : n * UNIT].rearrange("p (t w) -> p t w", t=n),
+            )
+
+        def store_out(ts, lo, hi):
+            cs = slice(lo * UNIT, hi * UNIT)
+            nc.sync.dma_start(out_rows[:, ts, cs], result[:, ts, cs])
+
+        def group_out(u):
+            cs = slice(u * UNIT, (u + 1) * UNIT)
+            nc.vector.tensor_copy(
+                out=o_grouped[:, cs, :].rearrange("p (c i) t -> p c t i", i=4),
+                in_=result[:, :, cs].rearrange("p t (c i) -> p c t i", i=4),
+            )
+
+        def quantise_out(c):
+            cs = slice(c * CHUNK, (c + 1) * CHUNK)
+            nc.vector.quantize_mx(
+                out=o_codes[:, cs].bitcast(FP8X4),
+                scales=o_scale[:, cs],
+                in_=o_grouped[:, cs, :].rearrange("p w t -> p (w t)"),
+            )
+
+        def store_words(lo, hi):
+            cs = slice(lo * CHUNK, hi * CHUNK)
+            nc.sync.dma_start(out_words[:, cs], o_codes[:, cs].bitcast(I32))
+
+        every = slice(0, PACK)
+        out_from = {1: 1, 2: 2, 3: 3, 4: 4, 6: 5, 7: 7}
+        words_from = {0: 0, 1: 1, 3: 2}
+        for half in range(2):
+            acc = bank(half)
+            ts = slice(2 * half, 2 * half + 2)
+            mix(acc, range(ts.start, ts.stop), 0)
+            copy_out(acc, ts, 0)
+            store_out(ts, 0, 1)
+        group_out(0)
+        for u in range(1, UNITS - 1):
+            acc = bank(u + 1)
+            mix(acc, range(PACK), u)
+            copy_out(acc, every, u)
+            if u in out_from:
+                store_out(every, out_from[u], u + 1)
+            group_out(u)
+            if u % 2 == 0:
+                c = u // 2 - 1
+                quantise_out(c)
+                if c in words_from:
+                    store_words(words_from[c], c + 1)
+        u = UNITS - 1
+        acc = bank(0)
+        mix(acc, range(PACK), u)
+        nc.scalar.copy(out=o_grouped[:, u * UNIT :, :], in_=acc[:].rearrange("p (t w) -> p w t", t=PACK))
+        quantise_out(CHUNKS - 1)
+        store_words(words_from[CHUNKS - 1], CHUNKS)
+        copy_out(acc, every, u)
+        store_out(every, out_from[u], UNITS)
         out_scale_rows = out_2[0].bitcast(I32)
         for r in range(4):
-            queue = nc.sync if r < 2 else nc.scalar
-            queue.dma_start(out_scale_rows[r:16:4, :], o_scale[r:P:32, :].bitcast(I32))
+            nc.sync.dma_start(out_scale_rows[r:16:4, :], o_scale[r:P:32, :].bitcast(I32))

@@ -24,7 +24,7 @@ UNIT = 128
 UNITS = U // UNIT
 HALF = S // 2
 FIRST = 128
-W1_HALF = 64
+W1_SPLIT = 64
 VECTOR_SLOTS = 640
 ORDER = (0, 1, 2, 3)
 
@@ -49,28 +49,26 @@ def tile_picked_pagemix_silu_po_kernel(
 
         x_table = sb([P, T], U32, "x_table")
         x_scale_table = sb([P, T], U8, "x_scale_table")
-        w1_raw = [sb([P, PACK, H // 2], F32, f"w1_raw{h}") for h in range(2)]
+        w1_raw = sb([P, PACK, H], F32, "w1_raw")
         w2_raw = sb([P, N], U32, "w2_raw")
         w2_scale_raw = sb([P, N], U8, "w2_scale_raw")
         page = [sb([P, U], F32, f"page{t}") for t in range(PACK)]
 
-        nc.vector.memset(x_scale_table[:].bitcast(I32), 0)
         nc.vector.memset(w2_scale_raw[:].bitcast(I32), 0)
+        nc.vector.memset(x_scale_table[:].bitcast(I32), 0)
 
         mem_rows = mem.rearrange("(p t) w -> t p w", t=PACK)
-        w1_rows = w1.rearrange("(p j) c -> p j c", j=PACK)
         x_scale_rows = x_scales[0].bitcast(I32)
         nc.sync.dma_start(offs_t[:], offs)
-        nc.sync.dma_start(w1_raw[0][:], w1_rows[:, :, : H // 2])
+        nc.sync.dma_start(w1_raw[:], w1.rearrange("(p j) c -> p j c", j=PACK))
         for r in range(4):
             nc.sync.dma_start(x_scale_table[r:P:32, :].bitcast(I32), x_scale_rows[r:16:4, :])
-        nc.sync.dma_start(w1_raw[1][:], w1_rows[:, :, H // 2 :])
         nc.scalar.dma_start(w2_scale_raw[0:16, :].bitcast(I32), w2_scales[0].bitcast(I32))
         nc.sync.dma_start(x_table[:].bitcast(I32), x_words[0].rearrange("p n t -> p (n t)").bitcast(I32))
         nc.sync.dma_start(slot_t[:], slot)
-        nc.sync.dma_start(page[ORDER[0]][:], mem_rows[ORDER[0]])
+        nc.sync.dma_start(page[0][:], mem_rows[0])
         nc.sync.dma_start(w2_raw[:].bitcast(I32), w2_words[0].rearrange("p n t -> p (n t)").bitcast(I32))
-        for t in ORDER[1:]:
+        for t in range(1, PACK):
             nc.sync.dma_start(page[t][:], mem_rows[t])
 
         w2_scale = sb([P, N], U8, "w2_scale")
@@ -80,14 +78,21 @@ def tile_picked_pagemix_silu_po_kernel(
         )
         w1_grouped = sb([P, H * PACK], BF16, "w1_grouped")
         w1_dst = w1_grouped[:].rearrange("p (t m j) -> p m j t", t=PACK, j=PACK)
-        w1_src = [w1_raw[h][:].rearrange("p j (m t) -> p m j t", t=PACK) for h in range(2)]
-        nc.scalar.copy(out=w1_dst[:, :W1_HALF], in_=w1_src[0])
-        x_scale = sb([P, S], U8, "x_scale")
-        nc.vector.tensor_copy(x_scale[:], x_scale_table[:].indirect(offs_t[:]))
-        nc.vector.tensor_copy(out=w1_dst[:, W1_HALF:], in_=w1_src[1])
+        w1_src = w1_raw[:].rearrange("p j (m t) -> p m j t", t=PACK)
+        nc.vector.tensor_copy(out=w1_dst[:, :W1_SPLIT], in_=w1_src[:, :W1_SPLIT])
+        nc.scalar.copy(out=w1_dst[:, W1_SPLIT:], in_=w1_src[:, W1_SPLIT:])
         w1_codes = sb([P, H], U32, "w1_codes")
         w1_scale = sb([P, H], U8, "w1_scale")
-        nc.vector.quantize_mx(out=w1_codes[:].bitcast(FP8X4), scales=w1_scale[:], in_=w1_grouped[:])
+        def quantise_w1(lo, hi):
+            nc.vector.quantize_mx(
+                out=w1_codes[:, lo:hi].bitcast(FP8X4),
+                scales=w1_scale[:, lo:hi],
+                in_=w1_grouped[:, lo * PACK : hi * PACK],
+            )
+
+        quantise_w1(0, P)
+        x_scale = sb([P, S], U8, "x_scale")
+        nc.vector.tensor_copy(x_scale[:], x_scale_table[:].indirect(offs_t[:]))
 
         x_codes = sb([P, S], U32, "x_codes")
         for h in range(2):
@@ -96,6 +101,8 @@ def tile_picked_pagemix_silu_po_kernel(
                 x_table[:].indirect(offs_t[:, h * HALF // 16 : (h + 1) * HALF // 16]),
             )
 
+        quantise_w1(P, 2 * P)
+        quantise_w1(2 * P, H)
         for q in range(1, QUADS):
             nc.sync.dma_start(
                 w2_scale[32 * q : 32 * q + 4, :].bitcast(I32), w2_scale[4 * q : 4 * q + 4, :].bitcast(I32)
@@ -146,7 +153,7 @@ def tile_picked_pagemix_silu_po_kernel(
             if t == ORDER[1]:
                 nc.scalar.copy(out=z_grouped[:, :, t], in_=page[t][:])
             if t == ORDER[2]:
-                for lo, hi in ((0, CHUNK), (CHUNK, 2 * CHUNK), (2 * CHUNK, VECTOR_SLOTS)):
+                for lo, hi in ((0, CHUNK), (CHUNK, CHUNK + UNIT), (CHUNK + UNIT, VECTOR_SLOTS)):
                     nc.scalar.copy(
                         out=z_grouped[:, lo:hi, t : t + 2],
                         in_=page[t][:, lo:hi].rearrange("p (w o) -> p w o", o=1).to_broadcast([P, hi - lo, 2]),
@@ -166,96 +173,78 @@ def tile_picked_pagemix_silu_po_kernel(
                 in_=z_grouped[:, lo:hi, :].rearrange("p w t -> p (w t)"),
             )
 
-        round_last(nc.vector.tensor_copy, 0, UNIT)
-        round_last(nc.vector.tensor_copy, UNIT, CHUNK)
+        round_last(nc.vector.tensor_copy, 0, CHUNK)
+        round_last(nc.vector.tensor_copy, CHUNK, CHUNK + UNIT)
         round_last(nc.scalar.copy, VECTOR_SLOTS, U)
-        quantise_z(0, UNIT)
-        round_last(nc.vector.tensor_copy, CHUNK, 2 * CHUNK)
-        quantise_z(UNIT, CHUNK)
-        round_last(nc.vector.tensor_copy, 2 * CHUNK, VECTOR_SLOTS)
-        quantise_z(CHUNK, 2 * CHUNK)
-        quantise_z(2 * CHUNK, U)
+        quantise_z(0, CHUNK)
+        round_last(nc.vector.tensor_copy, CHUNK + UNIT, VECTOR_SLOTS)
+        quantise_z(CHUNK, U - CHUNK)
+        quantise_z(U - CHUNK, U)
 
         out_rows = out_0.rearrange("(p t) w -> p t w", t=PACK)
         out_words = out_1[0].rearrange("p n t -> p (n t)").bitcast(I32)
         o_codes = sb([P, U], U32, "o_codes")
         o_scale = sb([P, U], U8, "o_scale")
-        result = sb([P, PACK, U], F32, "result")
-        o_grouped = sb([P, U, PACK], BF16, "o_grouped")
+        spans = ((0, CHUNK), (CHUNK, U - CHUNK), (U - CHUNK, U))
+        result = {lo: sb([P, PACK, hi - lo], F32, f"result{lo}") for lo, hi in spans}
+        o_grouped = [sb([P, CHUNK, PACK], BF16, f"o_grouped{c}") for c in range(CHUNKS)]
 
-        def mix(acc, planes, u):
-            cs = slice(u * UNIT, (u + 1) * UNIT)
-            for i, t in enumerate(planes):
+        def hand_out(b, engine_copy, first_plane, end_plane, lo, hi):
+            acc = bank(b % 8)
+            width = hi - lo
+            planes = slice(first_plane, end_plane)
+            for i, t in enumerate(range(first_plane, end_plane)):
                 nc.tensor.matmul_mx(
-                    out=acc[:, i * UNIT : (i + 1) * UNIT],
+                    out=acc[:, i * width : (i + 1) * width],
                     lhsT=w2_codes[:, t * P : (t + 1) * P].bitcast(FP8X4),
                     lhsT_scale=w2_scale[:, t * P : (t + 1) * P],
-                    rhs=z_codes[:, cs].bitcast(FP8X4),
-                    rhs_scale=z_scale[:, cs],
+                    rhs=z_codes[:, lo:hi].bitcast(FP8X4),
+                    rhs_scale=z_scale[:, lo:hi],
                     start=True,
                     stop=True,
                 )
+            count = end_plane - first_plane
+            engine_copy(
+                out=result[lo][:, planes, :], in_=acc[:, : count * width].rearrange("p (t w) -> p t w", t=count)
+            )
+            nc.sync.dma_start(out_rows[:, planes, lo:hi], result[lo][:, planes, :])
 
-        def copy_out(acc, ts, u):
-            n = ts.stop - ts.start
-            nc.scalar.copy(
-                out=result[:, ts, u * UNIT : (u + 1) * UNIT],
-                in_=acc[:, : n * UNIT].rearrange("p (t w) -> p t w", t=n),
+        def group_out(engine_copy, start, lo, hi):
+            engine_copy(
+                out=o_grouped[lo // CHUNK][:].rearrange("p (c i) t -> p c t i", i=4),
+                in_=result[start][:, :, lo - start : hi - start].rearrange("p t (c i) -> p c t i", i=4),
             )
 
-        def store_out(ts, lo, hi):
-            cs = slice(lo * UNIT, hi * UNIT)
-            nc.sync.dma_start(out_rows[:, ts, cs], result[:, ts, cs])
-
-        def group_out(u):
-            cs = slice(u * UNIT, (u + 1) * UNIT)
-            nc.vector.tensor_copy(
-                out=o_grouped[:, cs, :].rearrange("p (c i) t -> p c t i", i=4),
-                in_=result[:, :, cs].rearrange("p t (c i) -> p c t i", i=4),
-            )
-
-        def quantise_out(c):
-            cs = slice(c * CHUNK, (c + 1) * CHUNK)
+        def quantise_out(lo, hi):
             nc.vector.quantize_mx(
-                out=o_codes[:, cs].bitcast(FP8X4),
-                scales=o_scale[:, cs],
-                in_=o_grouped[:, cs, :].rearrange("p w t -> p (w t)"),
+                out=o_codes[:, lo:hi].bitcast(FP8X4),
+                scales=o_scale[:, lo:hi],
+                in_=o_grouped[lo // CHUNK][:].rearrange("p w t -> p (w t)"),
             )
 
         def store_words(lo, hi):
-            cs = slice(lo * CHUNK, hi * CHUNK)
-            nc.sync.dma_start(out_words[:, cs], o_codes[:, cs].bitcast(I32))
+            nc.sync.dma_start(out_words[:, lo:hi], o_codes[:, lo:hi].bitcast(I32))
 
-        every = slice(0, PACK)
-        out_from = {1: 1, 2: 2, 3: 3, 4: 4, 6: 5, 7: 7}
-        words_from = {0: 0, 1: 1, 3: 2}
-        for half in range(2):
-            acc = bank(half)
-            ts = slice(2 * half, 2 * half + 2)
-            mix(acc, range(ts.start, ts.stop), 0)
-            copy_out(acc, ts, 0)
-            store_out(ts, 0, 1)
-        group_out(0)
-        for u in range(1, UNITS - 1):
-            acc = bank(u + 1)
-            mix(acc, range(PACK), u)
-            copy_out(acc, every, u)
-            if u in out_from:
-                store_out(every, out_from[u], u + 1)
-            group_out(u)
-            if u % 2 == 0:
-                c = u // 2 - 1
-                quantise_out(c)
-                if c in words_from:
-                    store_words(words_from[c], c + 1)
-        u = UNITS - 1
-        acc = bank(0)
-        mix(acc, range(PACK), u)
-        nc.scalar.copy(out=o_grouped[:, u * UNIT :, :], in_=acc[:].rearrange("p (t w) -> p w t", t=PACK))
-        quantise_out(CHUNKS - 1)
-        store_words(words_from[CHUNKS - 1], CHUNKS)
-        copy_out(acc, every, u)
-        store_out(every, out_from[u], UNITS)
+        scalar, vector = nc.scalar.copy, nc.vector.tensor_copy
+        mid = U - CHUNK
+        hand_out(0, scalar, 0, 1, 0, CHUNK)
+        hand_out(1, scalar, 1, 2, 0, CHUNK)
+        hand_out(2, scalar, 2, 4, 0, CHUNK)
+        group_out(vector, 0, 0, CHUNK)
+        quantise_out(0, CHUNK)
+        for t in range(PACK):
+            hand_out(3 + t, vector if t == PACK - 1 else scalar, t, t + 1, CHUNK, mid)
+            if t == 1:
+                store_words(0, CHUNK)
+        hand_out(7, scalar, 0, 2, mid, U)
+        hand_out(8, scalar, 2, 4, mid, U)
+        group_out(vector, CHUNK, CHUNK, 2 * CHUNK)
+        group_out(vector, CHUNK, 2 * CHUNK, mid)
+        group_out(scalar, mid, mid, U)
+        quantise_out(CHUNK, 2 * CHUNK)
+        quantise_out(2 * CHUNK, mid)
+        quantise_out(mid, U)
+        store_words(CHUNK, U)
         out_scale_rows = out_2[0].bitcast(I32)
         for r in range(4):
-            nc.sync.dma_start(out_scale_rows[r:16:4, :], o_scale[r:P:32, :].bitcast(I32))
+            nc.scalar.dma_start(out_scale_rows[r:16:4, :], o_scale[r:P:32, :].bitcast(I32))

@@ -153,7 +153,7 @@ def tile_picked_pagemix_silu_po_kernel(
             if t == ORDER[1]:
                 nc.scalar.copy(out=z_grouped[:, :, t], in_=page[t][:])
             if t == ORDER[2]:
-                for lo, hi in ((0, CHUNK), (CHUNK, CHUNK + UNIT), (CHUNK + UNIT, VECTOR_SLOTS)):
+                for lo, hi in ((0, CHUNK), (CHUNK, 2 * CHUNK), (2 * CHUNK, VECTOR_SLOTS)):
                     nc.scalar.copy(
                         out=z_grouped[:, lo:hi, t : t + 2],
                         in_=page[t][:, lo:hi].rearrange("p (w o) -> p w o", o=1).to_broadcast([P, hi - lo, 2]),
@@ -173,78 +173,86 @@ def tile_picked_pagemix_silu_po_kernel(
                 in_=z_grouped[:, lo:hi, :].rearrange("p w t -> p (w t)"),
             )
 
-        round_last(nc.vector.tensor_copy, 0, CHUNK)
-        round_last(nc.vector.tensor_copy, CHUNK, CHUNK + UNIT)
+        round_last(nc.vector.tensor_copy, 0, UNIT)
+        round_last(nc.vector.tensor_copy, UNIT, CHUNK)
         round_last(nc.scalar.copy, VECTOR_SLOTS, U)
-        quantise_z(0, CHUNK)
-        round_last(nc.vector.tensor_copy, CHUNK + UNIT, VECTOR_SLOTS)
-        quantise_z(CHUNK, U - CHUNK)
-        quantise_z(U - CHUNK, U)
+        quantise_z(0, UNIT)
+        round_last(nc.vector.tensor_copy, CHUNK, 2 * CHUNK)
+        quantise_z(UNIT, CHUNK)
+        round_last(nc.vector.tensor_copy, 2 * CHUNK, VECTOR_SLOTS)
+        quantise_z(CHUNK, 2 * CHUNK)
+        quantise_z(2 * CHUNK, U)
 
         out_rows = out_0.rearrange("(p t) w -> p t w", t=PACK)
         out_words = out_1[0].rearrange("p n t -> p (n t)").bitcast(I32)
         o_codes = sb([P, U], U32, "o_codes")
         o_scale = sb([P, U], U8, "o_scale")
-        spans = ((0, CHUNK), (CHUNK, U - CHUNK), (U - CHUNK, U))
+        spans = ((0, CHUNK), (CHUNK, 2 * CHUNK), (2 * CHUNK, U))
         result = {lo: sb([P, PACK, hi - lo], F32, f"result{lo}") for lo, hi in spans}
         o_grouped = [sb([P, CHUNK, PACK], BF16, f"o_grouped{c}") for c in range(CHUNKS)]
 
-        def hand_out(b, engine_copy, first_plane, end_plane, lo, hi):
-            acc = bank(b % 8)
+        def mix(acc, first_plane, end_plane, lo, hi, part):
+            width = hi - lo
+            for start in range(0, width, part):
+                for i, t in enumerate(range(first_plane, end_plane)):
+                    nc.tensor.matmul_mx(
+                        out=acc[:, i * width + start : i * width + start + part],
+                        lhsT=w2_codes[:, t * P : (t + 1) * P].bitcast(FP8X4),
+                        lhsT_scale=w2_scale[:, t * P : (t + 1) * P],
+                        rhs=z_codes[:, lo + start : lo + start + part].bitcast(FP8X4),
+                        rhs_scale=z_scale[:, lo + start : lo + start + part],
+                        start=True,
+                        stop=True,
+                    )
+
+        def hand_out(b, engine_copy, first_plane, end_plane, lo, hi, part):
+            acc = bank(b)
             width = hi - lo
             planes = slice(first_plane, end_plane)
-            for i, t in enumerate(range(first_plane, end_plane)):
-                nc.tensor.matmul_mx(
-                    out=acc[:, i * width : (i + 1) * width],
-                    lhsT=w2_codes[:, t * P : (t + 1) * P].bitcast(FP8X4),
-                    lhsT_scale=w2_scale[:, t * P : (t + 1) * P],
-                    rhs=z_codes[:, lo:hi].bitcast(FP8X4),
-                    rhs_scale=z_scale[:, lo:hi],
-                    start=True,
-                    stop=True,
-                )
+            mix(acc, first_plane, end_plane, lo, hi, part)
             count = end_plane - first_plane
             engine_copy(
                 out=result[lo][:, planes, :], in_=acc[:, : count * width].rearrange("p (t w) -> p t w", t=count)
             )
             nc.sync.dma_start(out_rows[:, planes, lo:hi], result[lo][:, planes, :])
 
-        def group_out(engine_copy, start, lo, hi):
+        def group_out(engine_copy, start, c):
+            lo = c * CHUNK - start
             engine_copy(
-                out=o_grouped[lo // CHUNK][:].rearrange("p (c i) t -> p c t i", i=4),
-                in_=result[start][:, :, lo - start : hi - start].rearrange("p t (c i) -> p c t i", i=4),
+                out=o_grouped[c][:].rearrange("p (c i) t -> p c t i", i=4),
+                in_=result[start][:, :, lo : lo + CHUNK].rearrange("p t (c i) -> p c t i", i=4),
             )
 
-        def quantise_out(lo, hi):
+        def quantise_out(c):
+            cs = slice(c * CHUNK, (c + 1) * CHUNK)
             nc.vector.quantize_mx(
-                out=o_codes[:, lo:hi].bitcast(FP8X4),
-                scales=o_scale[:, lo:hi],
-                in_=o_grouped[lo // CHUNK][:].rearrange("p w t -> p (w t)"),
+                out=o_codes[:, cs].bitcast(FP8X4),
+                scales=o_scale[:, cs],
+                in_=o_grouped[c][:].rearrange("p w t -> p (w t)"),
             )
 
         def store_words(lo, hi):
             nc.sync.dma_start(out_words[:, lo:hi], o_codes[:, lo:hi].bitcast(I32))
 
         scalar, vector = nc.scalar.copy, nc.vector.tensor_copy
-        mid = U - CHUNK
-        hand_out(0, scalar, 0, 1, 0, CHUNK)
-        hand_out(1, scalar, 1, 2, 0, CHUNK)
-        hand_out(2, scalar, 2, 4, 0, CHUNK)
-        group_out(vector, 0, 0, CHUNK)
-        quantise_out(0, CHUNK)
+        mid = 2 * CHUNK
+        hand_out(0, scalar, 0, 1, 0, CHUNK, UNIT)
+        hand_out(1, scalar, 1, 2, 0, CHUNK, UNIT)
+        hand_out(2, vector, 2, 4, 0, CHUNK, UNIT)
+        hand_out(3, scalar, 0, 2, CHUNK, mid, CHUNK)
+        hand_out(4, scalar, 2, 4, CHUNK, mid, CHUNK)
+        group_out(vector, 0, 0)
+        quantise_out(0)
+        group_out(vector, CHUNK, 1)
         for t in range(PACK):
-            hand_out(3 + t, vector if t == PACK - 1 else scalar, t, t + 1, CHUNK, mid)
-            if t == 1:
-                store_words(0, CHUNK)
-        hand_out(7, scalar, 0, 2, mid, U)
-        hand_out(8, scalar, 2, 4, mid, U)
-        group_out(vector, CHUNK, CHUNK, 2 * CHUNK)
-        group_out(vector, CHUNK, 2 * CHUNK, mid)
-        group_out(scalar, mid, mid, U)
-        quantise_out(CHUNK, 2 * CHUNK)
-        quantise_out(2 * CHUNK, mid)
-        quantise_out(mid, U)
-        store_words(CHUNK, U)
+            hand_out((5 + t) % 8, vector if t == PACK - 1 else scalar, t, t + 1, mid, U, BANK)
+        quantise_out(1)
+        store_words(0, mid)
+        group_out(vector, mid, 2)
+        group_out(scalar, mid, 3)
+        quantise_out(2)
+        quantise_out(3)
+        store_words(mid, U)
         out_scale_rows = out_2[0].bitcast(I32)
         for r in range(4):
             nc.scalar.dma_start(out_scale_rows[r:16:4, :], o_scale[r:P:32, :].bitcast(I32))

@@ -126,6 +126,12 @@ def tile_picked_pagemix_silu_po_kernel(
         def scatter(t, y, lo, hi):
             nc.vector.tensor_copy(page[t][:].indirect(slot_t[:, lo // 16 : hi // 16]), y[:, lo:hi])
 
+        def whole_words(t, lo, hi):
+            nc.scalar.copy(
+                out=z_grouped[:, lo:hi, t : t + 2],
+                in_=page[t][:, lo:hi].rearrange("p (w o) -> p w o", o=1).to_broadcast([P, hi - lo, 2]),
+            )
+
         first = ORDER[0]
         y = {t: sb([P, S], F32, f"y{t}") for t in ORDER}
         acc = bank(7)
@@ -153,12 +159,10 @@ def tile_picked_pagemix_silu_po_kernel(
             if t == ORDER[1]:
                 nc.scalar.copy(out=z_grouped[:, :, t], in_=page[t][:])
             if t == ORDER[2]:
-                for lo, hi in ((0, CHUNK), (CHUNK, 2 * CHUNK), (2 * CHUNK, VECTOR_SLOTS)):
-                    nc.scalar.copy(
-                        out=z_grouped[:, lo:hi, t : t + 2],
-                        in_=page[t][:, lo:hi].rearrange("p (w o) -> p w o", o=1).to_broadcast([P, hi - lo, 2]),
-                    )
+                whole_words(t, 0, CHUNK)
                 nc.scalar.copy(out=z_grouped[:, VECTOR_SLOTS:, t], in_=page[t][:, VECTOR_SLOTS:])
+                whole_words(t, CHUNK, 2 * CHUNK)
+                whole_words(t, 2 * CHUNK, VECTOR_SLOTS)
 
         z_codes = sb([P, U], U32, "z_codes")
         z_scale = sb([P, U], U8, "z_scale")
@@ -177,8 +181,8 @@ def tile_picked_pagemix_silu_po_kernel(
         round_last(nc.vector.tensor_copy, UNIT, CHUNK)
         round_last(nc.scalar.copy, VECTOR_SLOTS, U)
         quantise_z(0, UNIT)
-        round_last(nc.vector.tensor_copy, CHUNK, 2 * CHUNK)
         quantise_z(UNIT, CHUNK)
+        round_last(nc.vector.tensor_copy, CHUNK, 2 * CHUNK)
         round_last(nc.vector.tensor_copy, 2 * CHUNK, VECTOR_SLOTS)
         quantise_z(CHUNK, 2 * CHUNK)
         quantise_z(2 * CHUNK, U)
@@ -237,15 +241,16 @@ def tile_picked_pagemix_silu_po_kernel(
         scalar, vector = nc.scalar.copy, nc.vector.tensor_copy
         mid = 2 * CHUNK
         hand_out(0, scalar, 0, 1, 0, CHUNK, UNIT)
-        hand_out(1, scalar, 1, 2, 0, CHUNK, UNIT)
-        hand_out(2, vector, 2, 4, 0, CHUNK, UNIT)
-        hand_out(3, scalar, 0, 2, CHUNK, mid, CHUNK)
-        hand_out(4, scalar, 2, 4, CHUNK, mid, CHUNK)
+        hand_out(1, scalar, 1, 2, 0, CHUNK, CHUNK)
+        hand_out(2, scalar, 2, 3, 0, CHUNK, CHUNK)
+        hand_out(3, vector, 3, 4, 0, CHUNK, CHUNK)
+        hand_out(4, scalar, 0, 2, CHUNK, mid, CHUNK)
+        hand_out(5, scalar, 2, 4, CHUNK, mid, CHUNK)
         group_out(vector, 0, 0)
         quantise_out(0)
         group_out(vector, CHUNK, 1)
         for t in range(PACK):
-            hand_out((5 + t) % 8, vector if t == PACK - 1 else scalar, t, t + 1, mid, U, BANK)
+            hand_out((6 + t) % 8, vector if t == PACK - 1 else scalar, t, t + 1, mid, U, BANK)
         quantise_out(1)
         store_words(0, mid)
         group_out(vector, mid, 2)

@@ -24,7 +24,8 @@ UNIT = 128
 UNITS = U // UNIT
 HALF = S // 2
 FIRST = 128
-W1_SPLIT = 64
+W1_SPLIT = 80
+ROWS_AT = 112
 VECTOR_SLOTS = 640
 ORDER = (0, 1, 2, 3)
 
@@ -36,6 +37,7 @@ def tile_picked_pagemix_silu_po_kernel(
     with ExitStack() as ctx:
         lists = ctx.enter_context(tc.tile_pool(name="lists", bufs=1))
         keep = ctx.enter_context(tc.tile_pool(name="keep", bufs=1))
+        reuse = ctx.enter_context(tc.tile_pool(name="reuse", bufs=1))
         psum = ctx.enter_context(tc.psum_pool(name="psum", bufs=1))
 
         offs_t = lists.tile([P, S // 16], U16, name="offs_t")
@@ -47,65 +49,72 @@ def tile_picked_pagemix_silu_po_kernel(
         def bank(b):
             return psum.tile([P, BANK], F32, name=f"bank{b}", tag=f"bank{b}")
 
-        x_table = sb([P, T], U32, "x_table")
-        x_scale_table = sb([P, T], U8, "x_scale_table")
-        w1_raw = sb([P, PACK, H], F32, "w1_raw")
-        w2_raw = sb([P, N], U32, "w2_raw")
-        w2_scale_raw = sb([P, N], U8, "w2_scale_raw")
-        page = [sb([P, U], F32, f"page{t}") for t in range(PACK)]
+        def shared(shape, dtype, name, offset):
+            return reuse.tile(shape, dtype, name=name, tag=name, align_bytes=64, offset=offset)
 
-        nc.vector.memset(w2_scale_raw[:].bitcast(I32), 0)
-        nc.vector.memset(x_scale_table[:].bitcast(I32), 0)
+        x_scale_table = shared([P, T], U8, "x_scale_table", 0)
+        w1_raw = shared([P, PACK, H], F32, "w1_raw", 4096)
+        x_table = shared([P, T], U32, "x_table", 12288)
+        w1_grouped = shared([P, H * PACK], BF16, "w1_grouped", 21504)
+        w2_scale_raw = sb([P, N], U8, "w2_scale_raw")
+        x_scale = sb([P, S], U8, "x_scale")
+
+        nc.vector.memset(x_scale_table[:ROWS_AT, :].bitcast(I32), 0)
+        nc.vector.memset(x_scale[:].bitcast(I32), 0)
+        nc.vector.memset(w2_scale_raw[:ROWS_AT, :].bitcast(I32), 0)
 
         mem_rows = mem.rearrange("(p t) w -> t p w", t=PACK)
-        x_scale_rows = x_scales[0].bitcast(I32)
         nc.sync.dma_start(offs_t[:], offs)
+        nc.scalar.dma_start(x_scale_table[ROWS_AT:, :].bitcast(I32), x_scales[0].bitcast(I32))
         nc.sync.dma_start(w1_raw[:], w1.rearrange("(p j) c -> p j c", j=PACK))
-        for r in range(4):
-            nc.sync.dma_start(x_scale_table[r:P:32, :].bitcast(I32), x_scale_rows[r:16:4, :])
-        nc.scalar.dma_start(w2_scale_raw[0:16, :].bitcast(I32), w2_scales[0].bitcast(I32))
         nc.sync.dma_start(x_table[:].bitcast(I32), x_words[0].rearrange("p n t -> p (n t)").bitcast(I32))
         nc.sync.dma_start(slot_t[:], slot)
-        nc.sync.dma_start(page[0][:], mem_rows[0])
-        nc.sync.dma_start(w2_raw[:].bitcast(I32), w2_words[0].rearrange("p n t -> p (n t)").bitcast(I32))
-        for t in range(1, PACK):
-            nc.sync.dma_start(page[t][:], mem_rows[t])
+        nc.scalar.dma_start(w2_scale_raw[ROWS_AT:, :].bitcast(I32), w2_scales[0].bitcast(I32))
 
-        w2_scale = sb([P, N], U8, "w2_scale")
+        x_scale_picked = sb([P, S], U8, "x_scale_picked")
+        nc.vector.tensor_copy(x_scale_picked[:], x_scale_table[:].indirect(offs_t[:]))
+        for q in range(QUADS):
+            nc.sync.dma_start(
+                x_scale[32 * q : 32 * q + 4, :].bitcast(I32),
+                x_scale_picked[ROWS_AT + 4 * q : ROWS_AT + 4 * q + 4, :].bitcast(I32),
+            )
+        page = [shared([P, U], F32, "page0", 0)]
+        nc.sync.dma_start(page[0][:], mem_rows[0])
+
+        w2_scale_dealt = sb([P, N], U8, "w2_scale_dealt")
         nc.vector.tensor_copy(
-            out=w2_scale[:].rearrange("p (t m) -> p m t", t=PACK),
+            out=w2_scale_dealt[:].rearrange("p (t m) -> p m t", t=PACK),
             in_=w2_scale_raw[:].rearrange("p (m t) -> p m t", t=PACK),
         )
-        w1_grouped = sb([P, H * PACK], BF16, "w1_grouped")
         w1_dst = w1_grouped[:].rearrange("p (t m j) -> p m j t", t=PACK, j=PACK)
         w1_src = w1_raw[:].rearrange("p j (m t) -> p m j t", t=PACK)
         nc.vector.tensor_copy(out=w1_dst[:, :W1_SPLIT], in_=w1_src[:, :W1_SPLIT])
         nc.scalar.copy(out=w1_dst[:, W1_SPLIT:], in_=w1_src[:, W1_SPLIT:])
         w1_codes = sb([P, H], U32, "w1_codes")
         w1_scale = sb([P, H], U8, "w1_scale")
-        def quantise_w1(lo, hi):
-            nc.vector.quantize_mx(
-                out=w1_codes[:, lo:hi].bitcast(FP8X4),
-                scales=w1_scale[:, lo:hi],
-                in_=w1_grouped[:, lo * PACK : hi * PACK],
-            )
+        nc.vector.quantize_mx(out=w1_codes[:].bitcast(FP8X4), scales=w1_scale[:], in_=w1_grouped[:])
 
-        quantise_w1(0, P)
-        x_scale = sb([P, S], U8, "x_scale")
-        nc.vector.tensor_copy(x_scale[:], x_scale_table[:].indirect(offs_t[:]))
+        w2_raw = shared([P, N], U32, "w2_raw", 4096)
+        nc.sync.dma_start(w2_raw[:].bitcast(I32), w2_words[0].rearrange("p n t -> p (n t)").bitcast(I32))
+        page.append(shared([P, U], F32, "page1", 6144))
+        nc.sync.dma_start(page[1][:], mem_rows[1])
 
-        x_codes = sb([P, S], U32, "x_codes")
+        x_codes = shared([P, S], U32, "x_codes", 21504)
         for h in range(2):
             nc.vector.tensor_copy(
                 x_codes[:, h * HALF : (h + 1) * HALF],
                 x_table[:].indirect(offs_t[:, h * HALF // 16 : (h + 1) * HALF // 16]),
             )
 
-        quantise_w1(P, 2 * P)
-        quantise_w1(2 * P, H)
-        for q in range(1, QUADS):
+        w2_scale = shared([P, N], U8, "w2_scale", 12288)
+        nc.vector.memset(w2_scale[:].bitcast(I32), 0)
+        for t in range(2, PACK):
+            page.append(shared([P, U], F32, f"page{t}", 12800 + 4096 * (t - 2)))
+            nc.sync.dma_start(page[t][:], mem_rows[t])
+        for q in range(QUADS):
             nc.sync.dma_start(
-                w2_scale[32 * q : 32 * q + 4, :].bitcast(I32), w2_scale[4 * q : 4 * q + 4, :].bitcast(I32)
+                w2_scale[32 * q : 32 * q + 4, :].bitcast(I32),
+                w2_scale_dealt[ROWS_AT + 4 * q : ROWS_AT + 4 * q + 4, :].bitcast(I32),
             )
 
         w2_codes = sb([P, N], U32, "w2_codes")
@@ -148,11 +157,11 @@ def tile_picked_pagemix_silu_po_kernel(
             nc.scalar.activation(y[t][:], accs[t][:], SILU)
 
         scatter(first, y[first], 0, FIRST)
-        nc.vector.tensor_copy(
-            out=w2_codes[:].bitcast(I32).rearrange("p (t m) -> p m t", t=PACK),
-            in_=w2_raw[:].bitcast(I32).rearrange("p (m t) -> p m t", t=PACK),
-        )
         scatter(first, y[first], FIRST, S)
+        nc.scalar.copy(
+            out=w2_codes[:].rearrange("p (t m) -> p m t", t=PACK),
+            in_=w2_raw[:].rearrange("p (m t) -> p m t", t=PACK),
+        )
         nc.scalar.copy(out=z_grouped[:, :, first], in_=page[first][:])
         for t in ORDER[1:]:
             scatter(t, y[t], 0, S)

@@ -24,9 +24,9 @@ UNIT = 128
 UNITS = U // UNIT
 HALF = S // 2
 FIRST = 128
-W1_SPLIT = 80
+W1_SPLIT = 86
 ROWS_AT = 112
-VECTOR_SLOTS = 640
+VECTOR_SLOTS = 704
 ORDER = (0, 1, 2, 3)
 
 
@@ -224,10 +224,10 @@ def tile_picked_pagemix_silu_po_kernel(
             planes = slice(first_plane, end_plane)
             mix(acc, first_plane, end_plane, lo, hi, part)
             count = end_plane - first_plane
-            engine_copy(
-                out=result[lo][:, planes, :], in_=acc[:, : count * width].rearrange("p (t w) -> p t w", t=count)
-            )
-            nc.sync.dma_start(out_rows[:, planes, lo:hi], result[lo][:, planes, :])
+            start = max(s for s in result if s <= lo)
+            held = result[start][:, planes, lo - start : hi - start]
+            engine_copy(out=held, in_=acc[:, : count * width].rearrange("p (t w) -> p t w", t=count))
+            nc.sync.dma_start(out_rows[:, planes, lo:hi], held)
 
         def group_out(engine_copy, start, c):
             lo = c * CHUNK - start
@@ -249,17 +249,18 @@ def tile_picked_pagemix_silu_po_kernel(
 
         scalar, vector = nc.scalar.copy, nc.vector.tensor_copy
         mid = 2 * CHUNK
-        hand_out(0, scalar, 0, 1, 0, CHUNK, UNIT)
-        hand_out(1, scalar, 1, 2, 0, CHUNK, CHUNK)
-        hand_out(2, scalar, 2, 3, 0, CHUNK, CHUNK)
-        hand_out(3, vector, 3, 4, 0, CHUNK, CHUNK)
-        hand_out(4, scalar, 0, 2, CHUNK, mid, CHUNK)
-        hand_out(5, scalar, 2, 4, CHUNK, mid, CHUNK)
+        hand_out(0, scalar, 0, 1, 0, UNIT, UNIT)
+        hand_out(1, scalar, 1, 2, 0, CHUNK, UNIT)
+        hand_out(2, scalar, 0, 1, UNIT, CHUNK, UNIT)
+        hand_out(3, scalar, 2, 3, 0, CHUNK, CHUNK)
+        hand_out(4, vector, 3, 4, 0, CHUNK, CHUNK)
+        hand_out(5, scalar, 0, 2, CHUNK, mid, CHUNK)
+        hand_out(6, scalar, 2, 4, CHUNK, mid, CHUNK)
         group_out(vector, 0, 0)
         quantise_out(0)
         group_out(vector, CHUNK, 1)
         for t in range(PACK):
-            hand_out((6 + t) % 8, vector if t == PACK - 1 else scalar, t, t + 1, mid, U, BANK)
+            hand_out((7 + t) % 8, vector if t == PACK - 1 else scalar, t, t + 1, mid, U, BANK)
         quantise_out(1)
         store_words(0, mid)
         group_out(vector, mid, 2)

@@ -26,6 +26,7 @@ HALF = S // 2
 FIRST = 128
 W1_SPLIT = 86
 ROWS_AT = 112
+LAST_SPLIT = 80
 VECTOR_SLOTS = 704
 ORDER = (0, 1, 2, 3)
 
@@ -229,11 +230,11 @@ def tile_picked_pagemix_silu_po_kernel(
             engine_copy(out=held, in_=acc[:, : count * width].rearrange("p (t w) -> p t w", t=count))
             nc.sync.dma_start(out_rows[:, planes, lo:hi], held)
 
-        def group_out(engine_copy, start, c):
+        def group_out(engine_copy, start, c, first_slot=0, end_slot=CHUNK):
             lo = c * CHUNK - start
             engine_copy(
-                out=o_grouped[c][:].rearrange("p (c i) t -> p c t i", i=4),
-                in_=result[start][:, :, lo : lo + CHUNK].rearrange("p t (c i) -> p c t i", i=4),
+                out=o_grouped[c][:, first_slot:end_slot].rearrange("p (c i) t -> p c t i", i=4),
+                in_=result[start][:, :, lo + first_slot : lo + end_slot].rearrange("p t (c i) -> p c t i", i=4),
             )
 
         def quantise_out(c):
@@ -249,9 +250,8 @@ def tile_picked_pagemix_silu_po_kernel(
 
         scalar, vector = nc.scalar.copy, nc.vector.tensor_copy
         mid = 2 * CHUNK
-        hand_out(0, scalar, 0, 1, 0, UNIT, UNIT)
-        hand_out(1, scalar, 1, 2, 0, CHUNK, UNIT)
-        hand_out(2, scalar, 0, 1, UNIT, CHUNK, UNIT)
+        hand_out(0, scalar, 0, 1, 0, CHUNK, UNIT)
+        hand_out(1, scalar, 1, 2, 0, CHUNK, CHUNK)
         hand_out(3, scalar, 2, 3, 0, CHUNK, CHUNK)
         hand_out(4, vector, 3, 4, 0, CHUNK, CHUNK)
         hand_out(5, scalar, 0, 2, CHUNK, mid, CHUNK)
@@ -264,10 +264,12 @@ def tile_picked_pagemix_silu_po_kernel(
         quantise_out(1)
         store_words(0, mid)
         group_out(vector, mid, 2)
-        group_out(scalar, mid, 3)
+        group_out(scalar, mid, 3, LAST_SPLIT, CHUNK)
+        group_out(vector, mid, 3, 0, LAST_SPLIT)
         quantise_out(2)
         quantise_out(3)
         store_words(mid, U)
         out_scale_rows = out_2[0].bitcast(I32)
         for r in range(4):
-            nc.scalar.dma_start(out_scale_rows[r:16:4, :], o_scale[r:P:32, :].bitcast(I32))
+            queue = nc.sync if r == 3 else nc.scalar
+            queue.dma_start(out_scale_rows[r:16:4, :], o_scale[r:P:32, :].bitcast(I32))

@@ -219,7 +219,7 @@ def tile_picked_pagemix_silu_po_kernel(
                         stop=True,
                     )
 
-        def hand_out(b, engine_copy, first_plane, end_plane, lo, hi, part):
+        def hand_out(b, engine_copy, first_plane, end_plane, lo, hi, part, stored=True):
             acc = bank(b)
             width = hi - lo
             planes = slice(first_plane, end_plane)
@@ -228,7 +228,8 @@ def tile_picked_pagemix_silu_po_kernel(
             start = max(s for s in result if s <= lo)
             held = result[start][:, planes, lo - start : hi - start]
             engine_copy(out=held, in_=acc[:, : count * width].rearrange("p (t w) -> p t w", t=count))
-            nc.sync.dma_start(out_rows[:, planes, lo:hi], held)
+            if stored:
+                nc.sync.dma_start(out_rows[:, planes, lo:hi], held)
 
         def group_out(engine_copy, start, c, first_slot=0, end_slot=CHUNK):
             lo = c * CHUNK - start
@@ -250,8 +251,9 @@ def tile_picked_pagemix_silu_po_kernel(
 
         scalar, vector = nc.scalar.copy, nc.vector.tensor_copy
         mid = 2 * CHUNK
-        hand_out(0, scalar, 0, 1, 0, CHUNK, UNIT)
-        hand_out(1, scalar, 1, 2, 0, CHUNK, CHUNK)
+        hand_out(0, scalar, 0, 1, 0, UNIT, UNIT)
+        hand_out(1, scalar, 1, 2, 0, CHUNK, UNIT)
+        hand_out(2, scalar, 0, 1, UNIT, CHUNK, UNIT)
         hand_out(3, scalar, 2, 3, 0, CHUNK, CHUNK)
         hand_out(4, vector, 3, 4, 0, CHUNK, CHUNK)
         hand_out(5, scalar, 0, 2, CHUNK, mid, CHUNK)
@@ -260,7 +262,8 @@ def tile_picked_pagemix_silu_po_kernel(
         quantise_out(0)
         group_out(vector, CHUNK, 1)
         for t in range(PACK):
-            hand_out((7 + t) % 8, vector if t == PACK - 1 else scalar, t, t + 1, mid, U, BANK)
+            hand_out((7 + t) % 8, vector if t == PACK - 1 else scalar, t, t + 1, mid, U, BANK, t < 2)
+        nc.sync.dma_start(out_rows[:, 2:, mid:], result[mid][:, 2:, :])
         quantise_out(1)
         store_words(0, mid)
         group_out(vector, mid, 2)

@@ -118,7 +118,7 @@ def tile_picked_pagemix_silu_po_kernel(
                 w2_scale_dealt[ROWS_AT + 4 * q : ROWS_AT + 4 * q + 4, :].bitcast(I32),
             )
 
-        w2_codes = sb([P, N], U32, "w2_codes")
+        w2_codes = sb([P, N - P], U32, "w2_codes")
         z_grouped = sb([P, U, PACK], BF16, "z_grouped")
         last = ORDER[-1]
 
@@ -159,9 +159,9 @@ def tile_picked_pagemix_silu_po_kernel(
 
         scatter(first, y[first], 0, FIRST)
         scatter(first, y[first], FIRST, S)
+        w2_columns = w2_raw[:].rearrange("p (m t) -> p m t", t=PACK)
         nc.scalar.copy(
-            out=w2_codes[:].rearrange("p (t m) -> p m t", t=PACK),
-            in_=w2_raw[:].rearrange("p (m t) -> p m t", t=PACK),
+            out=w2_codes[:].rearrange("p (t m) -> p m t", t=PACK - 1), in_=w2_columns[:, :, : PACK - 1]
         )
         nc.scalar.copy(out=z_grouped[:, :, first], in_=page[first][:])
         for t in ORDER[1:]:
@@ -171,6 +171,19 @@ def tile_picked_pagemix_silu_po_kernel(
             if t == ORDER[2]:
                 whole_words(t, 0, CHUNK)
                 nc.scalar.copy(out=z_grouped[:, VECTOR_SLOTS:, t], in_=page[t][:, VECTOR_SLOTS:])
+                w2_last = sb([P, P], U32, "w2_last", tag=f"y{t}")
+                nc.scalar.copy(out=w2_last[:], in_=w2_columns[:, :, last])
+                warm = bank(2)
+                for i in range(2):
+                    nc.tensor.matmul_mx(
+                        out=warm[:],
+                        lhsT=w2_last[:].bitcast(FP8X4),
+                        lhsT_scale=w2_scale[:, last * P :],
+                        rhs=x_codes[:].bitcast(FP8X4),
+                        rhs_scale=x_scale[:],
+                        start=True,
+                        stop=True,
+                    )
                 whole_words(t, CHUNK, 2 * CHUNK)
                 whole_words(t, 2 * CHUNK, VECTOR_SLOTS)
 
@@ -211,7 +224,7 @@ def tile_picked_pagemix_silu_po_kernel(
                 for i, t in enumerate(range(first_plane, end_plane)):
                     nc.tensor.matmul_mx(
                         out=acc[:, i * width + start : i * width + start + part],
-                        lhsT=w2_codes[:, t * P : (t + 1) * P].bitcast(FP8X4),
+                        lhsT=(w2_last[:] if t == last else w2_codes[:, t * P : (t + 1) * P]).bitcast(FP8X4),
                         lhsT_scale=w2_scale[:, t * P : (t + 1) * P],
                         rhs=z_codes[:, lo + start : lo + start + part].bitcast(FP8X4),
                         rhs_scale=z_scale[:, lo + start : lo + start + part],
@@ -255,7 +268,7 @@ def tile_picked_pagemix_silu_po_kernel(
         hand_out(1, scalar, 1, 2, 0, CHUNK, UNIT)
         hand_out(2, scalar, 0, 1, UNIT, CHUNK, UNIT)
         hand_out(3, scalar, 2, 3, 0, CHUNK, CHUNK)
-        hand_out(4, vector, 3, 4, 0, CHUNK, CHUNK)
+        hand_out(4, scalar, 3, 4, 0, CHUNK, CHUNK)
         hand_out(5, scalar, 0, 2, CHUNK, mid, CHUNK)
         hand_out(6, scalar, 2, 4, CHUNK, mid, CHUNK)
         group_out(vector, 0, 0)

@@ -173,17 +173,6 @@ def tile_picked_pagemix_silu_po_kernel(
                 nc.scalar.copy(out=z_grouped[:, VECTOR_SLOTS:, t], in_=page[t][:, VECTOR_SLOTS:])
                 w2_last = sb([P, P], U32, "w2_last", tag=f"y{t}")
                 nc.scalar.copy(out=w2_last[:], in_=w2_columns[:, :, last])
-                warm = bank(2)
-                for i in range(2):
-                    nc.tensor.matmul_mx(
-                        out=warm[:],
-                        lhsT=w2_last[:].bitcast(FP8X4),
-                        lhsT_scale=w2_scale[:, last * P :],
-                        rhs=x_codes[:].bitcast(FP8X4),
-                        rhs_scale=x_scale[:],
-                        start=True,
-                        stop=True,
-                    )
                 whole_words(t, CHUNK, 2 * CHUNK)
                 whole_words(t, 2 * CHUNK, VECTOR_SLOTS)
 

@@ -21,14 +21,10 @@ BANK = 512
 CHUNK = 256
 CHUNKS = U // CHUNK
 UNIT = 128
-UNITS = U // UNIT
 HALF = S // 2
-FIRST = 128
-W1_SPLIT = 86
 ROWS_AT = 112
 LAST_SPLIT = 80
 VECTOR_SLOTS = 704
-ORDER = (0, 1, 2, 3)
 
 
 def tile_picked_pagemix_silu_po_kernel(
@@ -44,8 +40,8 @@ def tile_picked_pagemix_silu_po_kernel(
         offs_t = lists.tile([P, S // 16], U16, name="offs_t")
         slot_t = lists.tile([P, S // 16], U16, name="slot_t")
 
-        def sb(shape, dtype, name, tag=None):
-            return keep.tile(shape, dtype, name=name, tag=tag or name, align_bytes=64)
+        def sb(shape, dtype, name):
+            return keep.tile(shape, dtype, name=name, tag=name, align_bytes=64)
 
         def bank(b):
             return psum.tile([P, BANK], F32, name=f"bank{b}", tag=f"bank{b}")
@@ -75,7 +71,7 @@ def tile_picked_pagemix_silu_po_kernel(
         x_scale_picked = sb([P, S], U8, "x_scale_picked")
         nc.vector.tensor_copy(x_scale_picked[:], x_scale_table[:].indirect(offs_t[:]))
         for q in range(QUADS):
-            nc.sync.dma_start(
+            nc.scalar.dma_start(
                 x_scale[32 * q : 32 * q + 4, :].bitcast(I32),
                 x_scale_picked[ROWS_AT + 4 * q : ROWS_AT + 4 * q + 4, :].bitcast(I32),
             )
@@ -89,23 +85,25 @@ def tile_picked_pagemix_silu_po_kernel(
         )
         w1_dst = w1_grouped[:].rearrange("p (t m j) -> p m j t", t=PACK, j=PACK)
         w1_src = w1_raw[:].rearrange("p j (m t) -> p m j t", t=PACK)
-        nc.vector.tensor_copy(out=w1_dst[:, :W1_SPLIT], in_=w1_src[:, :W1_SPLIT])
-        nc.scalar.copy(out=w1_dst[:, W1_SPLIT:], in_=w1_src[:, W1_SPLIT:])
         w1_codes = sb([P, H], U32, "w1_codes")
         w1_scale = sb([P, H], U8, "w1_scale")
-        nc.vector.quantize_mx(out=w1_codes[:].bitcast(FP8X4), scales=w1_scale[:], in_=w1_grouped[:])
+        nc.vector.tensor_copy(out=w1_dst[:, :, :, :2], in_=w1_src[:, :, :, :2])
+        nc.vector.tensor_copy(out=w1_dst[:, :, :, 2:], in_=w1_src[:, :, :, 2:])
+        for lo in (0, H // 2):
+            nc.vector.quantize_mx(
+                out=w1_codes[:, lo : lo + H // 2].bitcast(FP8X4),
+                scales=w1_scale[:, lo : lo + H // 2],
+                in_=w1_grouped[:, PACK * lo : PACK * (lo + H // 2)],
+            )
 
-        w2_raw = shared([P, N], U32, "w2_raw", 4096)
-        nc.sync.dma_start(w2_raw[:].bitcast(I32), w2_words[0].rearrange("p n t -> p (n t)").bitcast(I32))
-        page.append(shared([P, U], F32, "page1", 6144))
+        page.append(shared([P, U], F32, "page1", 4096))
         nc.sync.dma_start(page[1][:], mem_rows[1])
+        w2_raw = shared([P, N], U32, "w2_raw", 8192)
+        nc.sync.dma_start(w2_raw[:].bitcast(I32), w2_words[0].rearrange("p n t -> p (n t)").bitcast(I32))
 
         x_codes = shared([P, S], U32, "x_codes", 21504)
-        for h in range(2):
-            nc.vector.tensor_copy(
-                x_codes[:, h * HALF : (h + 1) * HALF],
-                x_table[:].indirect(offs_t[:, h * HALF // 16 : (h + 1) * HALF // 16]),
-            )
+        for lo, hi in ((0, UNIT), (UNIT, HALF), (HALF, S)):
+            nc.vector.tensor_copy(x_codes[:, lo:hi], x_table[:].indirect(offs_t[:, lo // 16 : hi // 16]))
 
         w2_scale = shared([P, N], U8, "w2_scale", 12288)
         nc.vector.memset(w2_scale[:].bitcast(I32), 0)
@@ -118,13 +116,13 @@ def tile_picked_pagemix_silu_po_kernel(
                 w2_scale_dealt[ROWS_AT + 4 * q : ROWS_AT + 4 * q + 4, :].bitcast(I32),
             )
 
-        w2_codes = sb([P, N - P], U32, "w2_codes")
+        w2_codes = sb([P, N], U32, "w2_codes")
         z_grouped = sb([P, U, PACK], BF16, "z_grouped")
-        last = ORDER[-1]
 
-        def product(t, acc, lo, hi):
+        def project(t, b, lo, hi, y):
+            acc = bank(b)
             nc.tensor.matmul_mx(
-                out=acc[:, lo:hi],
+                out=acc[:, : hi - lo],
                 lhsT=w1_codes[:, t * P : (t + 1) * P].bitcast(FP8X4),
                 lhsT_scale=w1_scale[:, t * P : (t + 1) * P],
                 rhs=x_codes[:, lo:hi].bitcast(FP8X4),
@@ -132,55 +130,56 @@ def tile_picked_pagemix_silu_po_kernel(
                 start=True,
                 stop=True,
             )
+            nc.scalar.activation(y, acc[:, : hi - lo], SILU)
 
         def scatter(t, y, lo, hi):
-            nc.vector.tensor_copy(page[t][:].indirect(slot_t[:, lo // 16 : hi // 16]), y[:, lo:hi])
+            nc.vector.tensor_copy(page[t][:].indirect(slot_t[:, lo // 16 : hi // 16]), y)
 
-        def whole_words(t, lo, hi):
-            nc.scalar.copy(
-                out=z_grouped[:, lo:hi, t : t + 2],
-                in_=page[t][:, lo:hi].rearrange("p (w o) -> p w o", o=1).to_broadcast([P, hi - lo, 2]),
+        def round_plane(engine_copy, t, lo, hi):
+            engine_copy(out=z_grouped[:, lo:hi, t], in_=page[t][:, lo:hi])
+
+        def gpsimd_round(out, in_):
+            nc.gpsimd.tensor_scalar(
+                out=out, in0=in_, scalar1=1.0, scalar2=0.0, op0=mybir.AluOpType.mult, op1=mybir.AluOpType.add
             )
 
-        first = ORDER[0]
-        y = {t: sb([P, S], F32, f"y{t}") for t in ORDER}
-        acc = bank(7)
-        product(first, acc, 0, FIRST)
-        nc.scalar.activation(y[first][:, :FIRST], acc[:, :FIRST], SILU)
-        acc = bank(6)
-        product(first, acc, FIRST, HALF)
-        product(first, acc, HALF, S)
-        nc.scalar.activation(y[first][:, FIRST:], acc[:, FIRST:], SILU)
-        accs = {}
-        for b, t in enumerate(ORDER[1:]):
-            accs[t] = bank(5 - b)
-            product(t, accs[t], 0, S)
-            nc.scalar.activation(y[t][:], accs[t][:], SILU)
-
-        scatter(first, y[first], 0, FIRST)
-        scatter(first, y[first], FIRST, S)
-        w2_columns = w2_raw[:].rearrange("p (m t) -> p m t", t=PACK)
+        y_first = shared([P, HALF], F32, "y_first", 27136)
+        y1 = sb([P, S], F32, "y1")
+        project(0, 0, 0, UNIT, y_first[:, :UNIT])
+        project(0, 1, UNIT, HALF, y_first[:, UNIT:])
+        project(1, 2, 0, S, y1[:])
+        scatter(0, y_first[:], 0, HALF)
+        scatter(1, y1[:], 0, S)
+        y2 = shared([P, S], F32, "y2", 25600)
+        project(2, 3, 0, S, y2[:])
+        y_second = shared([P, HALF], F32, "y_second", 27648)
+        project(0, 5, HALF, S, y_second[:])
+        y3 = sb([P, S], F32, "y3")
+        project(3, 4, 0, S, y3[:])
+        scatter(0, y_second[:], HALF, S)
         nc.scalar.copy(
-            out=w2_codes[:].rearrange("p (t m) -> p m t", t=PACK - 1), in_=w2_columns[:, :, : PACK - 1]
+            out=w2_codes[:].rearrange("p (t m) -> p m t", t=PACK), in_=w2_raw[:].rearrange("p (m t) -> p m t", t=PACK)
         )
-        nc.scalar.copy(out=z_grouped[:, :, first], in_=page[first][:])
-        for t in ORDER[1:]:
-            scatter(t, y[t], 0, S)
-            if t == ORDER[1]:
-                nc.scalar.copy(out=z_grouped[:, :, t], in_=page[t][:])
-            if t == ORDER[2]:
-                whole_words(t, 0, CHUNK)
-                nc.scalar.copy(out=z_grouped[:, VECTOR_SLOTS:, t], in_=page[t][:, VECTOR_SLOTS:])
-                w2_last = sb([P, P], U32, "w2_last", tag=f"y{t}")
-                nc.scalar.copy(out=w2_last[:], in_=w2_columns[:, :, last])
-                whole_words(t, CHUNK, 2 * CHUNK)
-                whole_words(t, 2 * CHUNK, VECTOR_SLOTS)
+        round_plane(nc.scalar.copy, 1, 0, VECTOR_SLOTS)
+        round_plane(gpsimd_round, 1, VECTOR_SLOTS, U)
+        scatter(2, y2[:], 0, S)
+        round_plane(nc.scalar.copy, 0, 0, VECTOR_SLOTS)
+        round_plane(gpsimd_round, 0, VECTOR_SLOTS, U)
+        scatter(3, y3[:], 0, S)
+
+        def whole_words(lo, hi):
+            nc.scalar.copy(
+                out=z_grouped[:, lo:hi, 2:],
+                in_=page[2][:, lo:hi].rearrange("p (w o) -> p w o", o=1).to_broadcast([P, hi - lo, 2]),
+            )
+
+        whole_words(0, CHUNK)
+        round_plane(nc.scalar.copy, 2, VECTOR_SLOTS, U)
+        whole_words(CHUNK, 2 * CHUNK)
+        whole_words(2 * CHUNK, VECTOR_SLOTS)
 
         z_codes = sb([P, U], U32, "z_codes")
         z_scale = sb([P, U], U8, "z_scale")
-
-        def round_last(engine_copy, lo, hi):
-            engine_copy(out=z_grouped[:, lo:hi, last], in_=page[last][:, lo:hi])
 
         def quantise_z(lo, hi):
             nc.vector.quantize_mx(
@@ -189,13 +188,14 @@ def tile_picked_pagemix_silu_po_kernel(
                 in_=z_grouped[:, lo:hi, :].rearrange("p w t -> p (w t)"),
             )
 
-        round_last(nc.vector.tensor_copy, 0, UNIT)
-        round_last(nc.vector.tensor_copy, UNIT, CHUNK)
-        round_last(nc.scalar.copy, VECTOR_SLOTS, U)
+        scalar, vector = nc.scalar.copy, nc.vector.tensor_copy
+        round_plane(vector, 3, 0, UNIT)
+        round_plane(vector, 3, UNIT, CHUNK)
+        round_plane(scalar, 3, VECTOR_SLOTS, U)
         quantise_z(0, UNIT)
         quantise_z(UNIT, CHUNK)
-        round_last(nc.vector.tensor_copy, CHUNK, 2 * CHUNK)
-        round_last(nc.vector.tensor_copy, 2 * CHUNK, VECTOR_SLOTS)
+        round_plane(vector, 3, CHUNK, 2 * CHUNK)
+        round_plane(vector, 3, 2 * CHUNK, VECTOR_SLOTS)
         quantise_z(CHUNK, 2 * CHUNK)
         quantise_z(2 * CHUNK, U)
 
@@ -207,25 +207,21 @@ def tile_picked_pagemix_silu_po_kernel(
         result = {lo: sb([P, PACK, hi - lo], F32, f"result{lo}") for lo, hi in spans}
         o_grouped = [sb([P, CHUNK, PACK], BF16, f"o_grouped{c}") for c in range(CHUNKS)]
 
-        def mix(acc, first_plane, end_plane, lo, hi, part):
+        def hand_out(b, engine_copy, first_plane, end_plane, lo, hi, part, stored=True):
+            acc = bank(b)
             width = hi - lo
+            planes = slice(first_plane, end_plane)
             for start in range(0, width, part):
                 for i, t in enumerate(range(first_plane, end_plane)):
                     nc.tensor.matmul_mx(
                         out=acc[:, i * width + start : i * width + start + part],
-                        lhsT=(w2_last[:] if t == last else w2_codes[:, t * P : (t + 1) * P]).bitcast(FP8X4),
+                        lhsT=w2_codes[:, t * P : (t + 1) * P].bitcast(FP8X4),
                         lhsT_scale=w2_scale[:, t * P : (t + 1) * P],
                         rhs=z_codes[:, lo + start : lo + start + part].bitcast(FP8X4),
                         rhs_scale=z_scale[:, lo + start : lo + start + part],
                         start=True,
                         stop=True,
                     )
-
-        def hand_out(b, engine_copy, first_plane, end_plane, lo, hi, part, stored=True):
-            acc = bank(b)
-            width = hi - lo
-            planes = slice(first_plane, end_plane)
-            mix(acc, first_plane, end_plane, lo, hi, part)
             count = end_plane - first_plane
             start = max(s for s in result if s <= lo)
             held = result[start][:, planes, lo - start : hi - start]
@@ -251,20 +247,19 @@ def tile_picked_pagemix_silu_po_kernel(
         def store_words(lo, hi):
             nc.sync.dma_start(out_words[:, lo:hi], o_codes[:, lo:hi].bitcast(I32))
 
-        scalar, vector = nc.scalar.copy, nc.vector.tensor_copy
         mid = 2 * CHUNK
-        hand_out(0, scalar, 0, 1, 0, UNIT, UNIT)
-        hand_out(1, scalar, 1, 2, 0, CHUNK, UNIT)
-        hand_out(2, scalar, 0, 1, UNIT, CHUNK, UNIT)
-        hand_out(3, scalar, 2, 3, 0, CHUNK, CHUNK)
-        hand_out(4, scalar, 3, 4, 0, CHUNK, CHUNK)
-        hand_out(5, scalar, 0, 2, CHUNK, mid, CHUNK)
-        hand_out(6, scalar, 2, 4, CHUNK, mid, CHUNK)
+        hand_out(5, scalar, 0, 1, 0, UNIT, UNIT)
+        hand_out(6, scalar, 1, 2, 0, CHUNK, UNIT)
+        hand_out(7, scalar, 0, 1, UNIT, CHUNK, UNIT)
+        hand_out(0, scalar, 2, 3, 0, CHUNK, CHUNK)
+        hand_out(1, scalar, 3, 4, 0, CHUNK, CHUNK)
+        hand_out(2, scalar, 0, 2, CHUNK, mid, CHUNK)
+        hand_out(3, scalar, 2, 4, CHUNK, mid, CHUNK)
         group_out(vector, 0, 0)
         quantise_out(0)
         group_out(vector, CHUNK, 1)
         for t in range(PACK):
-            hand_out((7 + t) % 8, vector if t == PACK - 1 else scalar, t, t + 1, mid, U, BANK, t < 2)
+            hand_out(4 + t, vector if t == PACK - 1 else scalar, t, t + 1, mid, U, BANK, t < 2)
         nc.sync.dma_start(out_rows[:, 2:, mid:], result[mid][:, 2:, :])
         quantise_out(1)
         store_words(0, mid)
@@ -274,6 +269,7 @@ def tile_picked_pagemix_silu_po_kernel(
         quantise_out(2)
         quantise_out(3)
         store_words(mid, U)
+
         out_scale_rows = out_2[0].bitcast(I32)
         for r in range(4):
             queue = nc.sync if r == 3 else nc.scalar

@@ -71,7 +71,7 @@ def tile_picked_pagemix_silu_po_kernel(
         x_scale_picked = sb([P, S], U8, "x_scale_picked")
         nc.vector.tensor_copy(x_scale_picked[:], x_scale_table[:].indirect(offs_t[:]))
         for q in range(QUADS):
-            nc.scalar.dma_start(
+            nc.sync.dma_start(
                 x_scale[32 * q : 32 * q + 4, :].bitcast(I32),
                 x_scale_picked[ROWS_AT + 4 * q : ROWS_AT + 4 * q + 4, :].bitcast(I32),
             )
@@ -87,14 +87,9 @@ def tile_picked_pagemix_silu_po_kernel(
         w1_src = w1_raw[:].rearrange("p j (m t) -> p m j t", t=PACK)
         w1_codes = sb([P, H], U32, "w1_codes")
         w1_scale = sb([P, H], U8, "w1_scale")
-        nc.vector.tensor_copy(out=w1_dst[:, :, :, :2], in_=w1_src[:, :, :, :2])
-        nc.vector.tensor_copy(out=w1_dst[:, :, :, 2:], in_=w1_src[:, :, :, 2:])
-        for lo in (0, H // 2):
-            nc.vector.quantize_mx(
-                out=w1_codes[:, lo : lo + H // 2].bitcast(FP8X4),
-                scales=w1_scale[:, lo : lo + H // 2],
-                in_=w1_grouped[:, PACK * lo : PACK * (lo + H // 2)],
-            )
+        nc.vector.tensor_copy(out=w1_dst[:, :96], in_=w1_src[:, :96])
+        nc.scalar.copy(out=w1_dst[:, 96:], in_=w1_src[:, 96:])
+        nc.vector.quantize_mx(out=w1_codes[:].bitcast(FP8X4), scales=w1_scale[:], in_=w1_grouped[:])
 
         page.append(shared([P, U], F32, "page1", 4096))
         nc.sync.dma_start(page[1][:], mem_rows[1])

@@ -19,7 +19,6 @@ PACK = 4
 QUADS = 4
 BANK = 512
 CHUNK = 256
-CHUNKS = U // CHUNK
 UNIT = 128
 HALF = S // 2
 ROWS_AT = 112
@@ -200,20 +199,21 @@ def tile_picked_pagemix_silu_po_kernel(
         o_scale = sb([P, U], U8, "o_scale")
         spans = ((0, CHUNK), (CHUNK, 2 * CHUNK), (2 * CHUNK, U))
         result = {lo: sb([P, PACK, hi - lo], F32, f"result{lo}") for lo, hi in spans}
-        o_grouped = [sb([P, CHUNK, PACK], BF16, f"o_grouped{c}") for c in range(CHUNKS)]
+        o_grouped = {lo: sb([P, hi - lo, PACK], BF16, f"o_grouped{lo}") for lo, hi in ((0, CHUNK), (CHUNK, 2 * CHUNK), (2 * CHUNK, 3 * CHUNK), (3 * CHUNK, U))}
 
-        def hand_out(b, engine_copy, first_plane, end_plane, lo, hi, part, stored=True):
+        def hand_out(b, engine_copy, first_plane, end_plane, *cuts, stored=True):
             acc = bank(b)
+            lo, hi = cuts[0], cuts[-1]
             width = hi - lo
             planes = slice(first_plane, end_plane)
-            for start in range(0, width, part):
+            for first, end in zip(cuts, cuts[1:]):
                 for i, t in enumerate(range(first_plane, end_plane)):
                     nc.tensor.matmul_mx(
-                        out=acc[:, i * width + start : i * width + start + part],
+                        out=acc[:, i * width + first - lo : i * width + end - lo],
                         lhsT=w2_codes[:, t * P : (t + 1) * P].bitcast(FP8X4),
                         lhsT_scale=w2_scale[:, t * P : (t + 1) * P],
-                        rhs=z_codes[:, lo + start : lo + start + part].bitcast(FP8X4),
-                        rhs_scale=z_scale[:, lo + start : lo + start + part],
+                        rhs=z_codes[:, first:end].bitcast(FP8X4),
+                        rhs_scale=z_scale[:, first:end],
                         start=True,
                         stop=True,
                     )
@@ -224,45 +224,45 @@ def tile_picked_pagemix_silu_po_kernel(
             if stored:
                 nc.sync.dma_start(out_rows[:, planes, lo:hi], held)
 
-        def group_out(engine_copy, start, c, first_slot=0, end_slot=CHUNK):
-            lo = c * CHUNK - start
+        def group_out(engine_copy, lo, hi):
+            start = max(s for s in result if s <= lo)
+            first = max(s for s in o_grouped if s <= lo)
             engine_copy(
-                out=o_grouped[c][:, first_slot:end_slot].rearrange("p (c i) t -> p c t i", i=4),
-                in_=result[start][:, :, lo + first_slot : lo + end_slot].rearrange("p t (c i) -> p c t i", i=4),
+                out=o_grouped[first][:, lo - first : hi - first].rearrange("p (c i) t -> p c t i", i=4),
+                in_=result[start][:, :, lo - start : hi - start].rearrange("p t (c i) -> p c t i", i=4),
             )
 
-        def quantise_out(c):
-            cs = slice(c * CHUNK, (c + 1) * CHUNK)
+        def quantise_out(lo, hi):
             nc.vector.quantize_mx(
-                out=o_codes[:, cs].bitcast(FP8X4),
-                scales=o_scale[:, cs],
-                in_=o_grouped[c][:].rearrange("p w t -> p (w t)"),
+                out=o_codes[:, lo:hi].bitcast(FP8X4),
+                scales=o_scale[:, lo:hi],
+                in_=o_grouped[lo][:].rearrange("p w t -> p (w t)"),
             )
 
         def store_words(lo, hi):
             nc.sync.dma_start(out_words[:, lo:hi], o_codes[:, lo:hi].bitcast(I32))
 
         mid = 2 * CHUNK
-        hand_out(5, scalar, 0, 1, 0, UNIT, UNIT)
-        hand_out(6, scalar, 1, 2, 0, CHUNK, UNIT)
-        hand_out(7, scalar, 0, 1, UNIT, CHUNK, UNIT)
-        hand_out(0, scalar, 2, 3, 0, CHUNK, CHUNK)
-        hand_out(1, scalar, 3, 4, 0, CHUNK, CHUNK)
-        hand_out(2, scalar, 0, 2, CHUNK, mid, CHUNK)
-        hand_out(3, scalar, 2, 4, CHUNK, mid, CHUNK)
-        group_out(vector, 0, 0)
-        quantise_out(0)
-        group_out(vector, CHUNK, 1)
+        hand_out(5, scalar, 0, 1, 0, UNIT, CHUNK)
+        hand_out(6, scalar, 1, 2, 0, UNIT, CHUNK)
+        hand_out(7, scalar, 2, 3, 0, CHUNK)
+        hand_out(0, scalar, 3, 4, 0, CHUNK)
         for t in range(PACK):
-            hand_out(4 + t, vector if t == PACK - 1 else scalar, t, t + 1, mid, U, BANK, t < 2)
+            hand_out(1 + t, scalar, t, t + 1, CHUNK, mid, stored=t < 2)
+        nc.sync.dma_start(out_rows[:, 2:, CHUNK:mid], result[CHUNK][:, 2:, :])
+        group_out(vector, 0, CHUNK)
+        quantise_out(0, CHUNK)
+        group_out(vector, CHUNK, mid)
+        for t in range(PACK):
+            hand_out((5 + t) % 8, vector if t == PACK - 1 else scalar, t, t + 1, mid, U, stored=t < 2)
         nc.sync.dma_start(out_rows[:, 2:, mid:], result[mid][:, 2:, :])
-        quantise_out(1)
+        quantise_out(CHUNK, mid)
         store_words(0, mid)
-        group_out(vector, mid, 2)
-        group_out(scalar, mid, 3, LAST_SPLIT, CHUNK)
-        group_out(vector, mid, 3, 0, LAST_SPLIT)
-        quantise_out(2)
-        quantise_out(3)
+        group_out(vector, mid, 3 * CHUNK)
+        group_out(scalar, 3 * CHUNK + LAST_SPLIT, U)
+        group_out(vector, 3 * CHUNK, 3 * CHUNK + LAST_SPLIT)
+        quantise_out(mid, 3 * CHUNK)
+        quantise_out(3 * CHUNK, U)
         store_words(mid, U)
 
         out_scale_rows = out_2[0].bitcast(I32)

@@ -22,8 +22,9 @@ CHUNK = 256
 UNIT = 128
 HALF = S // 2
 ROWS_AT = 112
-LAST_SPLIT = 80
-VECTOR_SLOTS = 704
+W1_SPLIT = 96
+VECTOR_END = 832
+GROUP_SPLIT = 848
 
 
 def tile_picked_pagemix_silu_po_kernel(
@@ -86,8 +87,8 @@ def tile_picked_pagemix_silu_po_kernel(
         w1_src = w1_raw[:].rearrange("p j (m t) -> p m j t", t=PACK)
         w1_codes = sb([P, H], U32, "w1_codes")
         w1_scale = sb([P, H], U8, "w1_scale")
-        nc.vector.tensor_copy(out=w1_dst[:, :96], in_=w1_src[:, :96])
-        nc.scalar.copy(out=w1_dst[:, 96:], in_=w1_src[:, 96:])
+        nc.vector.tensor_copy(out=w1_dst[:, :W1_SPLIT], in_=w1_src[:, :W1_SPLIT])
+        nc.scalar.copy(out=w1_dst[:, W1_SPLIT:], in_=w1_src[:, W1_SPLIT:])
         nc.vector.quantize_mx(out=w1_codes[:].bitcast(FP8X4), scales=w1_scale[:], in_=w1_grouped[:])
 
         page.append(shared([P, U], F32, "page1", 4096))
@@ -113,64 +114,73 @@ def tile_picked_pagemix_silu_po_kernel(
         w2_codes = sb([P, N], U32, "w2_codes")
         z_grouped = sb([P, U, PACK], BF16, "z_grouped")
 
-        def project(t, b, lo, hi, y):
+        def project(t, b, y, *cuts):
             acc = bank(b)
-            nc.tensor.matmul_mx(
-                out=acc[:, : hi - lo],
-                lhsT=w1_codes[:, t * P : (t + 1) * P].bitcast(FP8X4),
-                lhsT_scale=w1_scale[:, t * P : (t + 1) * P],
-                rhs=x_codes[:, lo:hi].bitcast(FP8X4),
-                rhs_scale=x_scale[:, lo:hi],
-                start=True,
-                stop=True,
-            )
+            lo, hi = cuts[0], cuts[-1]
+            for first, end in zip(cuts, cuts[1:]):
+                nc.tensor.matmul_mx(
+                    out=acc[:, first - lo : end - lo],
+                    lhsT=w1_codes[:, t * P : (t + 1) * P].bitcast(FP8X4),
+                    lhsT_scale=w1_scale[:, t * P : (t + 1) * P],
+                    rhs=x_codes[:, first:end].bitcast(FP8X4),
+                    rhs_scale=x_scale[:, first:end],
+                    start=True,
+                    stop=True,
+                )
             nc.scalar.activation(y, acc[:, : hi - lo], SILU)
 
         def scatter(t, y, lo, hi):
             nc.vector.tensor_copy(page[t][:].indirect(slot_t[:, lo // 16 : hi // 16]), y)
-
-        def round_plane(engine_copy, t, lo, hi):
-            engine_copy(out=z_grouped[:, lo:hi, t], in_=page[t][:, lo:hi])
 
         def gpsimd_round(out, in_):
             nc.gpsimd.tensor_scalar(
                 out=out, in0=in_, scalar1=1.0, scalar2=0.0, op0=mybir.AluOpType.mult, op1=mybir.AluOpType.add
             )
 
-        y_first = shared([P, HALF], F32, "y_first", 27136)
-        y1 = sb([P, S], F32, "y1")
-        project(0, 0, 0, UNIT, y_first[:, :UNIT])
-        project(0, 1, UNIT, HALF, y_first[:, UNIT:])
-        project(1, 2, 0, S, y1[:])
-        scatter(0, y_first[:], 0, HALF)
-        scatter(1, y1[:], 0, S)
-        y2 = shared([P, S], F32, "y2", 25600)
-        project(2, 3, 0, S, y2[:])
-        y_second = shared([P, HALF], F32, "y_second", 27648)
-        project(0, 5, HALF, S, y_second[:])
-        y3 = sb([P, S], F32, "y3")
-        project(3, 4, 0, S, y3[:])
-        scatter(0, y_second[:], HALF, S)
-        nc.scalar.copy(
-            out=w2_codes[:].rearrange("p (t m) -> p m t", t=PACK), in_=w2_raw[:].rearrange("p (m t) -> p m t", t=PACK)
-        )
-        round_plane(nc.scalar.copy, 1, 0, VECTOR_SLOTS)
-        round_plane(gpsimd_round, 1, VECTOR_SLOTS, U)
-        scatter(2, y2[:], 0, S)
-        round_plane(nc.scalar.copy, 0, 0, VECTOR_SLOTS)
-        round_plane(gpsimd_round, 0, VECTOR_SLOTS, U)
-        scatter(3, y3[:], 0, S)
+        scalar, vector = nc.scalar.copy, nc.vector.tensor_copy
 
-        def whole_words(lo, hi):
-            nc.scalar.copy(
+        def round_plane(engine_copy, t, lo, hi):
+            engine_copy(out=z_grouped[:, lo:hi, t], in_=page[t][:, lo:hi])
+
+        def whole_words(engine_copy, lo, hi):
+            engine_copy(
                 out=z_grouped[:, lo:hi, 2:],
                 in_=page[2][:, lo:hi].rearrange("p (w o) -> p w o", o=1).to_broadcast([P, hi - lo, 2]),
             )
 
-        whole_words(0, CHUNK)
-        round_plane(nc.scalar.copy, 2, VECTOR_SLOTS, U)
-        whole_words(CHUNK, 2 * CHUNK)
-        whole_words(2 * CHUNK, VECTOR_SLOTS)
+        y_first = shared([P, HALF], F32, "y_first", 27136)
+        y1 = sb([P, S], F32, "y1")
+        project(0, 0, y_first[:, :UNIT], 0, UNIT)
+        project(0, 1, y_first[:, UNIT:], UNIT, HALF)
+        project(1, 2, y1[:], 0, S)
+        scatter(0, y_first[:], 0, HALF)
+        scatter(1, y1[:], 0, S)
+        y2 = shared([P, S], F32, "y2", 25600)
+        project(2, 3, y2[:], 0, S)
+        y_second = shared([P, HALF], F32, "y_second", 27648)
+        project(0, 5, y_second[:], HALF, S)
+        y3 = sb([P, S], F32, "y3")
+        project(3, 4, y3[:], 0, S)
+        scatter(0, y_second[:], HALF, S)
+        nc.scalar.copy(
+            out=w2_codes[:].rearrange("p (t m) -> p m t", t=PACK), in_=w2_raw[:].rearrange("p (m t) -> p m t", t=PACK)
+        )
+        mid = 2 * CHUNK
+
+        def round_early(t):
+            round_plane(scalar, t, 0, CHUNK)
+            round_plane(gpsimd_round, t, CHUNK, mid)
+            round_plane(scalar, t, mid, U)
+
+        round_early(1)
+        scatter(2, y2[:], 0, S)
+        round_early(0)
+        scatter(3, y3[:], 0, S)
+
+        whole_words(scalar, 0, CHUNK)
+        whole_words(gpsimd_round, CHUNK, mid)
+        round_plane(scalar, 2, VECTOR_END, U)
+        whole_words(scalar, mid, VECTOR_END)
 
         z_codes = sb([P, U], U32, "z_codes")
         z_scale = sb([P, U], U8, "z_scale")
@@ -182,30 +192,30 @@ def tile_picked_pagemix_silu_po_kernel(
                 in_=z_grouped[:, lo:hi, :].rearrange("p w t -> p (w t)"),
             )
 
-        scalar, vector = nc.scalar.copy, nc.vector.tensor_copy
         round_plane(vector, 3, 0, UNIT)
         round_plane(vector, 3, UNIT, CHUNK)
-        round_plane(scalar, 3, VECTOR_SLOTS, U)
+        round_plane(scalar, 3, CHUNK, mid)
+        round_plane(scalar, 3, VECTOR_END, U)
         quantise_z(0, UNIT)
         quantise_z(UNIT, CHUNK)
-        round_plane(vector, 3, CHUNK, 2 * CHUNK)
-        round_plane(vector, 3, 2 * CHUNK, VECTOR_SLOTS)
-        quantise_z(CHUNK, 2 * CHUNK)
-        quantise_z(2 * CHUNK, U)
+        round_plane(vector, 3, mid, VECTOR_END)
+        quantise_z(CHUNK, mid)
+        quantise_z(mid, U)
 
         out_rows = out_0.rearrange("(p t) w -> p t w", t=PACK)
         out_words = out_1[0].rearrange("p n t -> p (n t)").bitcast(I32)
         o_codes = sb([P, U], U32, "o_codes")
         o_scale = sb([P, U], U8, "o_scale")
-        spans = ((0, CHUNK), (CHUNK, 2 * CHUNK), (2 * CHUNK, U))
-        result = {lo: sb([P, PACK, hi - lo], F32, f"result{lo}") for lo, hi in spans}
-        o_grouped = {lo: sb([P, hi - lo, PACK], BF16, f"o_grouped{lo}") for lo, hi in ((0, CHUNK), (CHUNK, 2 * CHUNK), (2 * CHUNK, 3 * CHUNK), (3 * CHUNK, U))}
+        result = {
+            0: sb([P, PACK, CHUNK], F32, "result_first"),
+            CHUNK: sb([P, PACK, U - CHUNK], F32, "result_rest"),
+        }
+        o_grouped = {lo: sb([P, hi - lo, PACK], BF16, f"o_grouped{lo}") for lo, hi in ((0, CHUNK), (CHUNK, mid), (mid, 3 * CHUNK), (3 * CHUNK, U))}
 
-        def hand_out(b, engine_copy, first_plane, end_plane, *cuts, stored=True):
+        def mix(b, engine_copy, first_plane, end_plane, *cuts):
             acc = bank(b)
             lo, hi = cuts[0], cuts[-1]
             width = hi - lo
-            planes = slice(first_plane, end_plane)
             for first, end in zip(cuts, cuts[1:]):
                 for i, t in enumerate(range(first_plane, end_plane)):
                     nc.tensor.matmul_mx(
@@ -219,10 +229,14 @@ def tile_picked_pagemix_silu_po_kernel(
                     )
             count = end_plane - first_plane
             start = max(s for s in result if s <= lo)
-            held = result[start][:, planes, lo - start : hi - start]
-            engine_copy(out=held, in_=acc[:, : count * width].rearrange("p (t w) -> p t w", t=count))
-            if stored:
-                nc.sync.dma_start(out_rows[:, planes, lo:hi], held)
+            engine_copy(
+                out=result[start][:, first_plane:end_plane, lo - start : hi - start],
+                in_=acc[:, : count * width].rearrange("p (t w) -> p t w", t=count),
+            )
+
+        def store(t, lo, hi):
+            start = max(s for s in result if s <= lo)
+            nc.sync.dma_start(out_rows[:, t, lo:hi], result[start][:, t, lo - start : hi - start])
 
         def group_out(engine_copy, lo, hi):
             start = max(s for s in result if s <= lo)
@@ -242,25 +256,30 @@ def tile_picked_pagemix_silu_po_kernel(
         def store_words(lo, hi):
             nc.sync.dma_start(out_words[:, lo:hi], o_codes[:, lo:hi].bitcast(I32))
 
-        mid = 2 * CHUNK
-        hand_out(5, scalar, 0, 1, 0, UNIT, CHUNK)
-        hand_out(6, scalar, 1, 2, 0, UNIT, CHUNK)
-        hand_out(7, scalar, 2, 3, 0, CHUNK)
-        hand_out(0, scalar, 3, 4, 0, CHUNK)
         for t in range(PACK):
-            hand_out(1 + t, scalar, t, t + 1, CHUNK, mid, stored=t < 2)
-        nc.sync.dma_start(out_rows[:, 2:, CHUNK:mid], result[CHUNK][:, 2:, :])
+            cuts = (0, UNIT, CHUNK) if t < 2 else (0, CHUNK)
+            mix((6 + t) % 8, scalar, t, t + 1, *cuts)
+            store(t, 0, CHUNK)
+        for t in range(2):
+            mix(2 + t, scalar if t else vector, t, t + 1, CHUNK, mid)
+            store(t, CHUNK, mid)
+        mix(4, scalar, 0, 1, mid, U)
+        store(0, mid, U)
         group_out(vector, 0, CHUNK)
+        mix(0, vector, 2, 4, CHUNK, mid)
         quantise_out(0, CHUNK)
-        group_out(vector, CHUNK, mid)
-        for t in range(PACK):
-            hand_out((5 + t) % 8, vector if t == PACK - 1 else scalar, t, t + 1, mid, U, stored=t < 2)
-        nc.sync.dma_start(out_rows[:, 2:, mid:], result[mid][:, 2:, :])
+        nc.vector.tensor_copy(out=o_grouped[CHUNK][:], in_=result[CHUNK][:, :, :CHUNK].rearrange("p t w -> p w t"))
+        mix(1, scalar, 1, 2, mid, U)
+        store(1, mid, U)
+        mix(3, scalar, 2, 3, mid, U)
+        store(2, CHUNK, U)
         quantise_out(CHUNK, mid)
         store_words(0, mid)
+        mix(4, scalar, 3, 4, mid, U)
+        store(3, CHUNK, U)
         group_out(vector, mid, 3 * CHUNK)
-        group_out(scalar, 3 * CHUNK + LAST_SPLIT, U)
-        group_out(vector, 3 * CHUNK, 3 * CHUNK + LAST_SPLIT)
+        group_out(scalar, GROUP_SPLIT, U)
+        group_out(vector, 3 * CHUNK, GROUP_SPLIT)
         quantise_out(mid, 3 * CHUNK)
         quantise_out(3 * CHUNK, U)
         store_words(mid, U)

@@ -25,6 +25,7 @@ ROWS_AT = 112
 W1_SPLIT = 96
 VECTOR_END = 832
 GROUP_SPLIT = 848
+STRIDE = BANK + PACK * CHUNK
 
 
 def tile_picked_pagemix_silu_po_kernel(
@@ -206,9 +207,12 @@ def tile_picked_pagemix_silu_po_kernel(
         out_words = out_1[0].rearrange("p n t -> p (n t)").bitcast(I32)
         o_codes = sb([P, U], U32, "o_codes")
         o_scale = sb([P, U], U8, "o_scale")
+        spread = sb([P, PACK * STRIDE], F32, "spread")
+        second_at = 2 * STRIDE + BANK
         result = {
-            0: sb([P, PACK, CHUNK], F32, "result_first"),
-            CHUNK: sb([P, PACK, U - CHUNK], F32, "result_rest"),
+            0: sb([P, PACK, CHUNK], F32, "result_first")[:],
+            CHUNK: spread[:, second_at : second_at + PACK * CHUNK].rearrange("p (t w) -> p t w", t=PACK),
+            mid: spread[:].rearrange("p (t s) -> p t s", t=PACK)[:, :, :BANK],
         }
         o_grouped = {lo: sb([P, hi - lo, PACK], BF16, f"o_grouped{lo}") for lo, hi in ((0, CHUNK), (CHUNK, mid), (mid, 3 * CHUNK), (3 * CHUNK, U))}
 
@@ -260,23 +264,22 @@ def tile_picked_pagemix_silu_po_kernel(
             cuts = (0, UNIT, CHUNK) if t < 2 else (0, CHUNK)
             mix((6 + t) % 8, scalar, t, t + 1, *cuts)
             store(t, 0, CHUNK)
-        for t in range(2):
-            mix(2 + t, scalar if t else vector, t, t + 1, CHUNK, mid)
+        for t, b in enumerate((2, 3, 5)):
+            mix(b, scalar if t else vector, t, t + 1, CHUNK, mid)
             store(t, CHUNK, mid)
         mix(4, scalar, 0, 1, mid, U)
         store(0, mid, U)
         group_out(vector, 0, CHUNK)
-        mix(0, vector, 2, 4, CHUNK, mid)
+        mix(0, vector, 3, 4, CHUNK, mid)
         quantise_out(0, CHUNK)
-        nc.vector.tensor_copy(out=o_grouped[CHUNK][:], in_=result[CHUNK][:, :, :CHUNK].rearrange("p t w -> p w t"))
-        mix(1, scalar, 1, 2, mid, U)
-        store(1, mid, U)
-        mix(3, scalar, 2, 3, mid, U)
-        store(2, CHUNK, U)
+        group_out(vector, CHUNK, mid)
+        mix(1, scalar, 3, 4, mid, U)
+        nc.sync.dma_start(out_rows[:, 3, CHUNK:], spread[:, 3 * STRIDE - CHUNK : 3 * STRIDE + BANK])
+        mix(5, vector, 2, 3, mid, U)
+        mix(3, scalar, 1, 2, mid, U)
+        nc.sync.dma_start(out_rows[:, 1:3, mid:], result[mid][:, 1:3, :])
         quantise_out(CHUNK, mid)
         store_words(0, mid)
-        mix(4, scalar, 3, 4, mid, U)
-        store(3, CHUNK, U)
         group_out(vector, mid, 3 * CHUNK)
         group_out(scalar, GROUP_SPLIT, U)
         group_out(vector, 3 * CHUNK, GROUP_SPLIT)

from contextlib import ExitStack

import concourse.mybir as mybir

K, T, S, N, U, H = 512, 2048, 512, 512, 1024, 512
FLOPS = 2 * K * H * S + 2 * H * N * U

F32 = mybir.dt.float32
BF16 = mybir.dt.bfloat16
I32 = mybir.dt.int32
U32 = mybir.dt.uint32
U16 = mybir.dt.uint16
U8 = mybir.dt.uint8
FP8X4 = mybir.dt.float8_e4m3fn_x4
SILU = mybir.ActivationFunctionType.Silu

P = 128
PACK = 4
QUADS = 4
BANK = 512
CHUNK = 256
UNIT = 128
HALF = S // 2
ROWS_AT = 112
W1_SPLIT = 96
VECTOR_END = 832
GROUP_SPLIT = 848
STRIDE = BANK + PACK * CHUNK


def tile_picked_pagemix_silu_po_kernel(
    tc, x_words, x_scales, w1, mem, w2_words, w2_scales, offs, slot, out_0, out_1, out_2
):
    nc = tc.nc
    with ExitStack() as ctx:
        lists = ctx.enter_context(tc.tile_pool(name="lists", bufs=1))
        keep = ctx.enter_context(tc.tile_pool(name="keep", bufs=1))
        reuse = ctx.enter_context(tc.tile_pool(name="reuse", bufs=1))
        psum = ctx.enter_context(tc.psum_pool(name="psum", bufs=1))

        offs_t = lists.tile([P, S // 16], U16, name="offs_t")
        slot_t = lists.tile([P, S // 16], U16, name="slot_t")

        def sb(shape, dtype, name):
            return keep.tile(shape, dtype, name=name, tag=name, align_bytes=64)

        def bank(b):
            return psum.tile([P, BANK], F32, name=f"bank{b}", tag=f"bank{b}")

        def shared(shape, dtype, name, offset):
            return reuse.tile(shape, dtype, name=name, tag=name, align_bytes=64, offset=offset)

        x_scale_table = shared([P, T], U8, "x_scale_table", 0)
        w1_raw = shared([P, PACK, H], F32, "w1_raw", 4096)
        x_table = shared([P, T], U32, "x_table", 12288)
        w1_grouped = shared([P, H * PACK], BF16, "w1_grouped", 21504)
        w2_scale_raw = sb([P, N], U8, "w2_scale_raw")
        x_scale = sb([P, S], U8, "x_scale")

        nc.vector.memset(x_scale_table[:ROWS_AT, :].bitcast(I32), 0)
        nc.vector.memset(x_scale[:].bitcast(I32), 0)
        nc.vector.memset(w2_scale_raw[:ROWS_AT, :].bitcast(I32), 0)

        mem_rows = mem.rearrange("(p t) w -> t p w", t=PACK)
        nc.sync.dma_start(offs_t[:], offs)
        nc.scalar.dma_start(x_scale_table[ROWS_AT:, :].bitcast(I32), x_scales[0].bitcast(I32))
        nc.sync.dma_start(w1_raw[:], w1.rearrange("(p j) c -> p j c", j=PACK))
        nc.sync.dma_start(x_table[:].bitcast(I32), x_words[0].rearrange("p n t -> p (n t)").bitcast(I32))
        nc.sync.dma_start(slot_t[:], slot)
        nc.scalar.dma_start(w2_scale_raw[ROWS_AT:, :].bitcast(I32), w2_scales[0].bitcast(I32))

        x_scale_picked = sb([P, S], U8, "x_scale_picked")
        nc.vector.tensor_copy(x_scale_picked[:], x_scale_table[:].indirect(offs_t[:]))
        for q in range(QUADS):
            nc.sync.dma_start(
                x_scale[32 * q : 32 * q + 4, :].bitcast(I32),
                x_scale_picked[ROWS_AT + 4 * q : ROWS_AT + 4 * q + 4, :].bitcast(I32),
            )
        page = [shared([P, U], F32, "page0", 0)]
        nc.sync.dma_start(page[0][:], mem_rows[0])

        w2_scale_dealt = sb([P, N], U8, "w2_scale_dealt")
        nc.vector.tensor_copy(
            out=w2_scale_dealt[:].rearrange("p (t m) -> p m t", t=PACK),
            in_=w2_scale_raw[:].rearrange("p (m t) -> p m t", t=PACK),
        )
        w1_dst = w1_grouped[:].rearrange("p (t m j) -> p m j t", t=PACK, j=PACK)
        w1_src = w1_raw[:].rearrange("p j (m t) -> p m j t", t=PACK)
        w1_codes = sb([P, H], U32, "w1_codes")
        w1_scale = sb([P, H], U8, "w1_scale")
        nc.vector.tensor_copy(out=w1_dst[:, :W1_SPLIT], in_=w1_src[:, :W1_SPLIT])
        nc.scalar.copy(out=w1_dst[:, W1_SPLIT:], in_=w1_src[:, W1_SPLIT:])
        nc.vector.quantize_mx(out=w1_codes[:].bitcast(FP8X4), scales=w1_scale[:], in_=w1_grouped[:])

        page.append(shared([P, U], F32, "page1", 4096))
        nc.sync.dma_start(page[1][:], mem_rows[1])
        w2_raw = shared([P, N], U32, "w2_raw", 8192)
        nc.sync.dma_start(w2_raw[:].bitcast(I32), w2_words[0].rearrange("p n t -> p (n t)").bitcast(I32))

        x_codes = shared([P, S], U32, "x_codes", 21504)
        for lo, hi in ((0, UNIT), (UNIT, HALF), (HALF, S)):
            nc.vector.tensor_copy(x_codes[:, lo:hi], x_table[:].indirect(offs_t[:, lo // 16 : hi // 16]))

        w2_scale = shared([P, N], U8, "w2_scale", 12288)
        nc.vector.memset(w2_scale[:].bitcast(I32), 0)
        for t in range(2, PACK):
            page.append(shared([P, U], F32, f"page{t}", 12800 + 4096 * (t - 2)))
            nc.sync.dma_start(page[t][:], mem_rows[t])
        for q in range(QUADS):
            nc.sync.dma_start(
                w2_scale[32 * q : 32 * q + 4, :].bitcast(I32),
                w2_scale_dealt[ROWS_AT + 4 * q : ROWS_AT + 4 * q + 4, :].bitcast(I32),
            )

        w2_codes = sb([P, N], U32, "w2_codes")
        z_grouped = sb([P, U, PACK], BF16, "z_grouped")

        def project(t, b, y, *cuts):
            acc = bank(b)
            lo, hi = cuts[0], cuts[-1]
            for first, end in zip(cuts, cuts[1:]):
                nc.tensor.matmul_mx(
                    out=acc[:, first - lo : end - lo],
                    lhsT=w1_codes[:, t * P : (t + 1) * P].bitcast(FP8X4),
                    lhsT_scale=w1_scale[:, t * P : (t + 1) * P],
                    rhs=x_codes[:, first:end].bitcast(FP8X4),
                    rhs_scale=x_scale[:, first:end],
                    start=True,
                    stop=True,
                )
            nc.scalar.activation(y, acc[:, : hi - lo], SILU)

        def scatter(t, y, lo, hi):
            nc.vector.tensor_copy(page[t][:].indirect(slot_t[:, lo // 16 : hi // 16]), y)

        def gpsimd_round(out, in_):
            nc.gpsimd.tensor_scalar(
                out=out, in0=in_, scalar1=1.0, scalar2=0.0, op0=mybir.AluOpType.mult, op1=mybir.AluOpType.add
            )

        scalar, vector = nc.scalar.copy, nc.vector.tensor_copy

        def round_plane(engine_copy, t, lo, hi):
            engine_copy(out=z_grouped[:, lo:hi, t], in_=page[t][:, lo:hi])

        def whole_words(engine_copy, lo, hi):
            engine_copy(
                out=z_grouped[:, lo:hi, 2:],
                in_=page[2][:, lo:hi].rearrange("p (w o) -> p w o", o=1).to_broadcast([P, hi - lo, 2]),
            )

        y_first = shared([P, HALF], F32, "y_first", 27136)
        y1 = sb([P, S], F32, "y1")
        project(0, 0, y_first[:, :UNIT], 0, UNIT)
        project(0, 1, y_first[:, UNIT:], UNIT, HALF)
        project(1, 2, y1[:], 0, S)
        scatter(0, y_first[:], 0, HALF)
        scatter(1, y1[:], 0, S)
        y2 = shared([P, S], F32, "y2", 25600)
        project(2, 3, y2[:], 0, S)
        y_second = shared([P, HALF], F32, "y_second", 27648)
        project(0, 5, y_second[:], HALF, S)
        y3 = sb([P, S], F32, "y3")
        project(3, 4, y3[:], 0, S)
        scatter(0, y_second[:], HALF, S)
        nc.scalar.copy(
            out=w2_codes[:].rearrange("p (t m) -> p m t", t=PACK), in_=w2_raw[:].rearrange("p (m t) -> p m t", t=PACK)
        )
        mid = 2 * CHUNK

        def round_early(t):
            round_plane(scalar, t, 0, CHUNK)
            round_plane(gpsimd_round, t, CHUNK, mid)
            round_plane(scalar, t, mid, U)

        round_early(1)
        scatter(2, y2[:], 0, S)
        round_early(0)
        scatter(3, y3[:], 0, S)

        whole_words(scalar, 0, CHUNK)
        whole_words(gpsimd_round, CHUNK, mid)
        round_plane(scalar, 2, VECTOR_END, U)
        whole_words(scalar, mid, VECTOR_END)

        z_codes = sb([P, U], U32, "z_codes")
        z_scale = sb([P, U], U8, "z_scale")

        def quantise_z(lo, hi):
            nc.vector.quantize_mx(
                out=z_codes[:, lo:hi].bitcast(FP8X4),
                scales=z_scale[:, lo:hi],
                in_=z_grouped[:, lo:hi, :].rearrange("p w t -> p (w t)"),
            )

        round_plane(vector, 3, 0, UNIT)
        round_plane(vector, 3, UNIT, CHUNK)
        round_plane(scalar, 3, CHUNK, mid)
        round_plane(scalar, 3, VECTOR_END, U)
        quantise_z(0, UNIT)
        quantise_z(UNIT, CHUNK)
        round_plane(vector, 3, mid, VECTOR_END)
        quantise_z(CHUNK, mid)
        quantise_z(mid, U)

        out_rows = out_0.rearrange("(p t) w -> p t w", t=PACK)
        out_words = out_1[0].rearrange("p n t -> p (n t)").bitcast(I32)
        o_codes = sb([P, U], U32, "o_codes")
        o_scale = sb([P, U], U8, "o_scale")
        spread = sb([P, PACK * STRIDE], F32, "spread")
        second_at = 2 * STRIDE + BANK
        result = {
            0: sb([P, PACK, CHUNK], F32, "result_first")[:],
            CHUNK: spread[:, second_at : second_at + PACK * CHUNK].rearrange("p (t w) -> p t w", t=PACK),
            mid: spread[:].rearrange("p (t s) -> p t s", t=PACK)[:, :, :BANK],
        }
        o_grouped = {lo: sb([P, hi - lo, PACK], BF16, f"o_grouped{lo}") for lo, hi in ((0, CHUNK), (CHUNK, mid), (mid, 3 * CHUNK), (3 * CHUNK, U))}

        def mix(b, engine_copy, first_plane, end_plane, *cuts):
            acc = bank(b)
            lo, hi = cuts[0], cuts[-1]
            width = hi - lo
            for first, end in zip(cuts, cuts[1:]):
                for i, t in enumerate(range(first_plane, end_plane)):
                    nc.tensor.matmul_mx(
                        out=acc[:, i * width + first - lo : i * width + end - lo],
                        lhsT=w2_codes[:, t * P : (t + 1) * P].bitcast(FP8X4),
                        lhsT_scale=w2_scale[:, t * P : (t + 1) * P],
                        rhs=z_codes[:, first:end].bitcast(FP8X4),
                        rhs_scale=z_scale[:, first:end],
                        start=True,
                        stop=True,
                    )
            count = end_plane - first_plane
            start = max(s for s in result if s <= lo)
            engine_copy(
                out=result[start][:, first_plane:end_plane, lo - start : hi - start],
                in_=acc[:, : count * width].rearrange("p (t w) -> p t w", t=count),
            )

        def store(t, lo, hi):
            start = max(s for s in result if s <= lo)
            nc.sync.dma_start(out_rows[:, t, lo:hi], result[start][:, t, lo - start : hi - start])

        def group_out(engine_copy, lo, hi):
            start = max(s for s in result if s <= lo)
            first = max(s for s in o_grouped if s <= lo)
            engine_copy(
                out=o_grouped[first][:, lo - first : hi - first].rearrange("p (c i) t -> p c t i", i=4),
                in_=result[start][:, :, lo - start : hi - start].rearrange("p t (c i) -> p c t i", i=4),
            )

        def quantise_out(lo, hi):
            nc.vector.quantize_mx(
                out=o_codes[:, lo:hi].bitcast(FP8X4),
                scales=o_scale[:, lo:hi],
                in_=o_grouped[lo][:].rearrange("p w t -> p (w t)"),
            )

        def store_words(lo, hi):
            nc.sync.dma_start(out_words[:, lo:hi], o_codes[:, lo:hi].bitcast(I32))

        for t in range(PACK):
            cuts = (0, UNIT, CHUNK) if t < 2 else (0, CHUNK)
            mix((6 + t) % 8, scalar, t, t + 1, *cuts)
            store(t, 0, CHUNK)
        for t, b in enumerate((2, 3, 5)):
            mix(b, scalar if t else vector, t, t + 1, CHUNK, mid)
            store(t, CHUNK, mid)
        mix(4, scalar, 0, 1, mid, U)
        store(0, mid, U)
        group_out(vector, 0, CHUNK)
        mix(0, vector, 3, 4, CHUNK, mid)
        quantise_out(0, CHUNK)
        group_out(vector, CHUNK, mid)
        mix(1, scalar, 3, 4, mid, U)
        nc.sync.dma_start(out_rows[:, 3, CHUNK:], spread[:, 3 * STRIDE - CHUNK : 3 * STRIDE + BANK])
        mix(5, vector, 2, 3, mid, U)
        mix(3, scalar, 1, 2, mid, U)
        nc.sync.dma_start(out_rows[:, 1:3, mid:], result[mid][:, 1:3, :])
        quantise_out(CHUNK, mid)
        store_words(0, mid)
        group_out(vector, mid, 3 * CHUNK)
        group_out(scalar, GROUP_SPLIT, U)
        group_out(vector, 3 * CHUNK, GROUP_SPLIT)
        quantise_out(mid, 3 * CHUNK)
        quantise_out(3 * CHUNK, U)
        store_words(mid, U)

        out_scale_rows = out_2[0].bitcast(I32)
        for r in range(4):
            queue = nc.sync if r == 3 else nc.scalar
            queue.dma_start(out_scale_rows[r:16:4, :], o_scale[r:P:32, :].bitcast(I32))
